import numpy as np
import ml_dtypes


def mxq(x, axis, fmt="e4m3"):
    dtype, down = {"e4m3": (ml_dtypes.float8_e4m3fn, 7), "e5m2": (ml_dtypes.float8_e5m2, 14)}[fmt]
    v = np.moveaxis(np.asarray(x, np.float32).astype(ml_dtypes.bfloat16).astype(np.float64), axis, -1)
    blocks = v.reshape(v.shape[:-1] + (-1, 32))
    amax = np.abs(blocks).max(-1, keepdims=True)
    byte = np.maximum(np.where(amax > 0, np.frexp(amax)[1] - 1 + 127, 0) - down, 1)
    scale = np.exp2(byte - 127.0)
    codes = (blocks / scale).astype(np.float32).astype(dtype).astype(np.float64)
    return np.moveaxis((codes * scale).reshape(v.shape), -1, axis)


WIDE = False


def mx_kscale(k):
    if not WIDE:
        return np.ones(k)
    levels = np.array([24, -24, 12, -12, 0])
    if k % 512:
        return np.exp2(np.random.permutation(np.resize(levels, k // 32))).repeat(32)
    a = np.empty((k // 512, 16))
    for p in range(k // 512):
        a[p, :8] = np.random.permutation(np.resize(levels, 8))
        for g in range(8):
            far = levels[np.abs(levels - a[p, g]) >= 10]
            a[p, g + 8] = far[np.random.randint(len(far))]
    return np.exp2(a.ravel()).repeat(32)


def f64(x):
    return np.asarray(x).astype(np.float64)


def striped(idx):
    return np.tile(idx.reshape(-1, 16).T, (8, 1)).astype(np.uint16)


def unstriped(offs):
    return offs[:16].T.reshape(-1).astype(np.int64)


E2M1 = np.array([0.0, 0.5, 1.0, 1.5, 2.0, 3.0, 4.0, 6.0, -0.0, -0.5, -1.0, -1.5, -2.0, -3.0, -4.0, -6.0])


def pack_weight(w, fmt):
    k, n = w.shape
    w = f64(np.asarray(w, np.float32).astype(ml_dtypes.bfloat16)).reshape(k // 32, 32, n)
    amax = np.abs(w).max(1)
    if fmt == "e4m3":
        byte = np.frexp(amax)[1] - 1 + 127 - 7
    else:
        mant, ex = np.frexp(amax / 6.0)
        byte = np.where(mant > 0.5, ex, ex - 1) + 127
    byte = np.clip(np.where(amax > 0, byte, 1), 1, 254)
    scaled = (w * np.exp2(127.0 - byte)[:, None, :]).reshape(k, n).astype(np.float32)
    by_word = np.ascontiguousarray(scaled.reshape(k // 512, 128, 4, n).transpose(0, 1, 3, 2))
    if fmt == "e4m3":
        words = by_word.astype(ml_dtypes.float8_e4m3fn).view(np.uint8)
    else:
        c = by_word.astype(ml_dtypes.float4_e2m1fn).view(np.uint8) & 0xF
        words = (c[..., 0::2] | (c[..., 1::2] << 4)).reshape(k // 512, 128, 2 * n)
    return np.ascontiguousarray(words), np.ascontiguousarray(byte.astype(np.uint8).reshape(k // 512, 16, n))


def unpack_weight(words, scales, fmt):
    g, _, n = scales.shape
    words = np.ascontiguousarray(words).reshape(g, 128, n, -1)
    if fmt == "e4m3":
        vals = words.view(ml_dtypes.float8_e4m3fn).astype(np.float64)
    else:
        nib = np.empty((g, 128, n, 4), np.uint8)
        nib[..., 0::2] = words & 0xF
        nib[..., 1::2] = words >> 4
        vals = E2M1[nib]
    vals = vals * np.repeat(np.exp2(scales.astype(np.float64) - 127.0), 8, axis=1)[..., None]
    return vals.transpose(0, 1, 3, 2).reshape(g * 512, n)


def planes(y):
    n, m = y.shape
    v = y.astype(np.float32).astype(ml_dtypes.bfloat16).astype(np.float64).reshape(n // 32, 32, m)
    top = np.abs(v).max(1)
    byte = np.clip(np.where(top > 0, np.frexp(top)[1] - 1 + 127 - 7, 1), 1, 254)
    codes = (v * np.exp2(127.0 - byte)[:, None, :]).reshape(n, m).astype(np.float32).astype(ml_dtypes.float8_e4m3fn).view(np.uint8)
    words = codes.reshape(n // 512, 128, 4, m).transpose(0, 1, 3, 2)
    return np.ascontiguousarray(words), np.ascontiguousarray(byte.astype(np.uint8).reshape(n // 512, 16, m))


K, R, N, T, J = 512, 512, 512, 2048, 1024


def setup_inputs():
    n = np.random.standard_normal
    s = mx_kscale(K)[:, None]
    u = mx_kscale(R)[:, None]
    p_tab = pack_weight(n((K, T)) * s, "e4m3")
    p_wd = pack_weight(n((R, N)) / np.sqrt(R) / u, "e2m1")
    return {
        "tab_words": p_tab[0],
        "tab_scales": p_tab[1],
        "wg": (n((K, R)) / np.sqrt(K) / s).astype(np.float32),
        "wu": (n((K, R)) / np.sqrt(K) / s * u.T).astype(np.float32),
        "wd_words": p_wd[0],
        "wd_scales": p_wd[1],
        "rT": (n((N, T))).astype(np.float32),
        "offs": striped(np.random.permutation(T)[:J]),
    }


def reference(tab_words, tab_scales, wg, wu, wd_words, wd_scales, rT, offs):
    idx = unstriped(offs)
    tab_ = unpack_weight(tab_words, tab_scales, "e4m3")[:, idx]
    wg_ = mxq(f64(wg), 0, "e4m3")
    wu_ = mxq(f64(wu), 0, "e4m3")
    ga = wg_.T @ tab_
    ub = wu_.T @ tab_
    h = np.maximum(ga, 0.0) * ub
    h_ = mxq(h, 0, "e4m3")
    wd_ = unpack_weight(wd_words, wd_scales, "e2m1")
    y = wd_.T @ h_
    out_0 = y + f64(rT)[:, idx]
    return (out_0,) + planes(out_0)

@@ -1,0 +1,207 @@
+from contextlib import ExitStack
+
+import concourse.mybir as mybir
+
+K, R, N, T, J = 512, 512, 512, 2048, 1024
+FLOPS = 2 * J * (2 * K * R + R * N)
+
+F32 = mybir.dt.float32
+BF16 = mybir.dt.bfloat16
+I32 = mybir.dt.int32
+U32 = mybir.dt.uint32
+U16 = mybir.dt.uint16
+U8 = mybir.dt.uint8
+FP8X4 = mybir.dt.float8_e4m3fn_x4
+FP4X4 = mybir.dt.float4_e2m1fn_x4
+ALU = mybir.AluOpType
+
+P = 128
+PACK = 4
+CHUNK = 128
+GROUP = 256
+LIST_ROWS = 16
+SCALAR_SHARE = 64
+HIDDEN_GROUP = 512
+OUT_WIDTHS = (256, 256, 256, 128, 128)
+
+
+def load_scale_rows(queue, plane, rows):
+    for q in range(4):
+        queue.dma_start(
+            out=plane[32 * q : 32 * q + 4, :].bitcast(I32),
+            in_=rows[4 * q : 4 * q + 4, :].bitcast(I32),
+        )
+
+
+def tile_list_gmlpt_relu_resLP_kernel(
+    tc, tab_words, tab_scales, wg, wu, wd_words, wd_scales, rT, offs, out_0, out_1, out_2
+):
+    nc = tc.nc
+    with ExitStack() as ctx:
+        keep = ctx.enter_context(tc.tile_pool(name="keep", bufs=1))
+        ring = ctx.enter_context(tc.tile_pool(name="ring", bufs=3))
+        psum_in = ctx.enter_context(tc.psum_pool(name="psum_in", bufs=2))
+        psum_out = ctx.enter_context(tc.psum_pool(name="psum_out", bufs=4))
+
+        offsets = keep.tile([P, J // LIST_ROWS], U16, name="offsets")
+        table_words = keep.tile([P, T], I32, name="table_words", align_bytes=64)
+        table_plane = keep.tile([P, T], U8, name="table_plane", align_bytes=64)
+        wg_raw = keep.tile([P, PACK, R], F32, name="wg_raw")
+        wu_raw = keep.tile([P, PACK, R], F32, name="wu_raw")
+        wd_raw = keep.tile([P, 2 * N], U8, name="wd_raw")
+        wd_plane_raw = keep.tile([P, N], U8, name="wd_plane_raw")
+        residual = [keep.tile([P, T], F32, name="residual%d" % t) for t in range(PACK)]
+
+        nc.gpsimd.memset(table_plane[:].bitcast(I32), 0)
+        nc.vector.memset(wd_plane_raw[:].bitcast(I32), 0)
+
+        nc.sync.dma_start(offsets[:], offs)
+        nc.sync.dma_start(out=wd_raw[:].bitcast(I32), in_=wd_words[0].bitcast(I32))
+        nc.sync.dma_start(
+            out=table_words[:], in_=tab_words[0].rearrange("p t i -> p (t i)").bitcast(I32)
+        )
+        load_scale_rows(nc.sync, table_plane, tab_scales[0])
+        nc.sync.dma_start(out=wg_raw[:], in_=wg.rearrange("(p i) r -> p i r", i=PACK))
+        nc.sync.dma_start(out=wu_raw[:], in_=wu.rearrange("(p i) r -> p i r", i=PACK))
+        load_scale_rows(nc.sync, wd_plane_raw, wd_scales[0])
+        residual_rows = rT.rearrange("(p t) c -> p t c", t=PACK)
+        for t in range(PACK):
+            nc.sync.dma_start(out=residual[t][:], in_=residual_rows[:, t, :])
+
+        wd_codes = keep.tile([P, PACK, 2 * P], U8, name="wd_codes", align_bytes=64)
+        nc.vector.tensor_copy(
+            wd_codes[:].rearrange("p t (m b) -> p m t b", b=2),
+            wd_raw[:].rearrange("p (m t b) -> p m t b", t=PACK, b=2),
+        )
+        picked_words = keep.tile([P, J], U32, name="picked_words", align_bytes=64)
+        nc.vector.tensor_copy(picked_words[:], table_words[:].bitcast(U32).indirect(offsets[:]))
+        picked_plane = keep.tile([P, J], U8, name="picked_plane", align_bytes=64)
+        nc.vector.tensor_copy(picked_plane[:], table_plane[:].indirect(offsets[:]))
+
+        def quantise_weight(raw, name, scalar_columns):
+            rounded = keep.tile([P, PACK * R], BF16, name=name + "_rounded", align_bytes=64)
+            codes = keep.tile([P, R], U32, name=name + "_codes", align_bytes=64)
+            plane = keep.tile([P, R], U8, name=name + "_plane", align_bytes=64)
+            dealt = rounded[:].rearrange("p (t m i) -> p m i t", t=PACK, i=PACK)
+            source = raw[:].rearrange("p i (m t) -> p m i t", t=PACK)
+            nc.scalar.copy(dealt[:, :scalar_columns], source[:, :scalar_columns])
+            if scalar_columns < P:
+                nc.vector.tensor_copy(dealt[:, scalar_columns:], source[:, scalar_columns:])
+            nc.vector.quantize_mx(out=codes[:].bitcast(FP8X4), scales=plane[:], in_=rounded[:])
+            return codes, plane
+
+        wg_codes, wg_plane = quantise_weight(wg_raw, "wg", P)
+        wu_codes, wu_plane = quantise_weight(wu_raw, "wu", SCALAR_SHARE)
+
+        wd_plane = keep.tile([P, PACK, P], U8, name="wd_plane", align_bytes=64)
+        nc.vector.tensor_copy(
+            wd_plane[:].rearrange("p t m -> p m t"),
+            wd_plane_raw[:].rearrange("p (m t) -> p m t", t=PACK),
+        )
+
+        def list_slice(first, count):
+            return offsets[:, first // LIST_ROWS : (first + count) // LIST_ROWS]
+
+        def four_slices(bank, codes_of, plane_of, moving, moving_plane):
+            for t in range(PACK):
+                nc.tensor.matmul_mx(
+                    out=bank[:, t, :],
+                    lhsT=codes_of(t),
+                    lhsT_scale=plane_of(t),
+                    rhs=moving,
+                    rhs_scale=moving_plane,
+                    start=True,
+                    stop=True,
+                )
+
+        h_codes = keep.tile([P, J], U32, name="h_codes", align_bytes=64)
+        h_plane = keep.tile([P, J], U8, name="h_plane", align_bytes=64)
+        for first in range(0, J, HIDDEN_GROUP):
+            h_rounded = ring.tile([P, HIDDEN_GROUP * PACK], BF16, name="h_rounded", align_bytes=64)
+            for c in range(HIDDEN_GROUP // CHUNK):
+                tokens = slice(first + c * CHUNK, first + (c + 1) * CHUNK)
+                moving = picked_words[:, tokens].bitcast(FP8X4)
+                moving_plane = picked_plane[:, tokens]
+                gate = psum_in.tile([P, PACK, CHUNK], F32, name="gate")
+                four_slices(
+                    gate,
+                    lambda t: wg_codes[:, t * P : (t + 1) * P].bitcast(FP8X4),
+                    lambda t: wg_plane[:, t * P : (t + 1) * P],
+                    moving,
+                    moving_plane,
+                )
+                up = psum_in.tile([P, PACK, CHUNK], F32, name="up")
+                four_slices(
+                    up,
+                    lambda t: wu_codes[:, t * P : (t + 1) * P].bitcast(FP8X4),
+                    lambda t: wu_plane[:, t * P : (t + 1) * P],
+                    moving,
+                    moving_plane,
+                )
+                gate_woven = ring.tile([P, CHUNK, PACK], F32, name="gate_woven")
+                nc.scalar.copy(gate_woven[:], gate[:].rearrange("p t j -> p j t"))
+                nc.vector.scalar_tensor_tensor(
+                    out=h_rounded[:, c * CHUNK * PACK : (c + 1) * CHUNK * PACK].rearrange(
+                        "p (j t) -> p j t", t=PACK
+                    ),
+                    in0=gate_woven[:],
+                    scalar=0.0,
+                    in1=up[:].rearrange("p t j -> p j t"),
+                    op0=ALU.max,
+                    op1=ALU.mult,
+                )
+            tokens = slice(first, first + HIDDEN_GROUP)
+            nc.vector.quantize_mx(
+                out=h_codes[:, tokens].bitcast(FP8X4), scales=h_plane[:, tokens], in_=h_rounded[:]
+            )
+
+        picked_residual = keep.tile([P, PACK, J], F32, name="picked_residual")
+        for t in range(PACK - 1):
+            nc.vector.tensor_copy(picked_residual[:, t, :], residual[t][:].indirect(offsets[:]))
+
+        out_plane = keep.tile([P, J], U8, name="out_plane", align_bytes=64)
+        out_rows = out_0.rearrange("(p t) j -> p t j", t=PACK)
+        out_words = out_1[0].rearrange("p j i -> p (j i)").bitcast(I32)
+        first = 0
+        for width in OUT_WIDTHS:
+            if first % GROUP == 0:
+                nc.vector.tensor_copy(
+                    picked_residual[:, PACK - 1, first : first + GROUP],
+                    residual[PACK - 1][:].indirect(list_slice(first, GROUP)),
+                )
+            result = keep.tile([P, PACK, width], F32, name="result%d" % first)
+            rounded = keep.tile([P, width * PACK], BF16, name="out_rounded%d" % first, align_bytes=64)
+            codes = keep.tile([P, width], I32, name="out_codes%d" % first, align_bytes=64)
+            for c in range(width // CHUNK):
+                cols = slice(c * CHUNK, (c + 1) * CHUNK)
+                tokens = slice(first + c * CHUNK, first + (c + 1) * CHUNK)
+                down = psum_out.tile([P, PACK, CHUNK], F32, name="down")
+                four_slices(
+                    down,
+                    lambda t: wd_codes[:, t, :].bitcast(FP4X4),
+                    lambda t: wd_plane[:, t, :],
+                    h_codes[:, tokens].bitcast(FP8X4),
+                    h_plane[:, tokens],
+                )
+                nc.vector.tensor_tensor(
+                    out=result[:, :, cols], in0=down[:], in1=picked_residual[:, :, tokens], op=ALU.add
+                )
+                nc.scalar.copy(
+                    rounded[:, c * CHUNK * PACK : (c + 1) * CHUNK * PACK].rearrange(
+                        "p (c i t) -> p c t i", i=4, t=PACK
+                    ),
+                    result[:, :, cols].rearrange("p t (c i) -> p c t i", i=4),
+                )
+            tokens = slice(first, first + width)
+            nc.sync.dma_start(out=out_rows[:, :, tokens], in_=result[:])
+            nc.vector.quantize_mx(
+                out=codes[:].bitcast(FP8X4), scales=out_plane[:, tokens], in_=rounded[:]
+            )
+            nc.sync.dma_start(out=out_words[:, tokens], in_=codes[:])
+            first = first + width
+        for q in range(4):
+            queue = nc.scalar if q % 2 == 0 else nc.sync
+            queue.dma_start(
+                out=out_2[0][4 * q : 4 * q + 4, :].bitcast(I32),
+                in_=out_plane[32 * q : 32 * q + 4, :].bitcast(I32),
+            )

@@ -22,7 +22,6 @@ GROUP = 256
 LIST_ROWS = 16
 SCALAR_SHARE = 64
 HIDDEN_GROUP = 512
-OUT_WIDTHS = (256, 256, 256, 128, 128)
 
 
 def load_scale_rows(queue, plane, rows):
@@ -39,9 +38,8 @@ def tile_list_gmlpt_relu_resLP_kernel(
     nc = tc.nc
     with ExitStack() as ctx:
         keep = ctx.enter_context(tc.tile_pool(name="keep", bufs=1))
-        ring = ctx.enter_context(tc.tile_pool(name="ring", bufs=3))
-        psum_in = ctx.enter_context(tc.psum_pool(name="psum_in", bufs=2))
-        psum_out = ctx.enter_context(tc.psum_pool(name="psum_out", bufs=4))
+        ring = ctx.enter_context(tc.tile_pool(name="ring", bufs=4))
+        psum = ctx.enter_context(tc.psum_pool(name="psum", bufs=4))
 
         offsets = keep.tile([P, J // LIST_ROWS], U16, name="offsets")
         table_words = keep.tile([P, T], I32, name="table_words", align_bytes=64)
@@ -52,8 +50,8 @@ def tile_list_gmlpt_relu_resLP_kernel(
         wd_plane_raw = keep.tile([P, N], U8, name="wd_plane_raw")
         residual = [keep.tile([P, T], F32, name="residual%d" % t) for t in range(PACK)]
 
-        nc.gpsimd.memset(table_plane[:].bitcast(I32), 0)
-        nc.vector.memset(wd_plane_raw[:].bitcast(I32), 0)
+        nc.vector.memset(table_plane[:].bitcast(I32), 0)
+        nc.gpsimd.memset(wd_plane_raw[:].bitcast(I32), 0)
 
         nc.sync.dma_start(offsets[:], offs)
         nc.sync.dma_start(out=wd_raw[:].bitcast(I32), in_=wd_words[0].bitcast(I32))
@@ -122,7 +120,7 @@ def tile_list_gmlpt_relu_resLP_kernel(
                 tokens = slice(first + c * CHUNK, first + (c + 1) * CHUNK)
                 moving = picked_words[:, tokens].bitcast(FP8X4)
                 moving_plane = picked_plane[:, tokens]
-                gate = psum_in.tile([P, PACK, CHUNK], F32, name="gate")
+                gate = psum.tile([P, PACK, CHUNK], F32, name="gate", tag="for_scalar")
                 four_slices(
                     gate,
                     lambda t: wg_codes[:, t * P : (t + 1) * P].bitcast(FP8X4),
@@ -130,7 +128,7 @@ def tile_list_gmlpt_relu_resLP_kernel(
                     moving,
                     moving_plane,
                 )
-                up = psum_in.tile([P, PACK, CHUNK], F32, name="up")
+                up = psum.tile([P, PACK, CHUNK], F32, name="up", tag="for_vector")
                 four_slices(
                     up,
                     lambda t: wu_codes[:, t * P : (t + 1) * P].bitcast(FP8X4),
@@ -155,50 +153,59 @@ def tile_list_gmlpt_relu_resLP_kernel(
                 out=h_codes[:, tokens].bitcast(FP8X4), scales=h_plane[:, tokens], in_=h_rounded[:]
             )
 
-        picked_residual = keep.tile([P, PACK, J], F32, name="picked_residual")
-        for t in range(PACK - 1):
-            nc.vector.tensor_copy(picked_residual[:, t, :], residual[t][:].indirect(offsets[:]))
+        down_rows = keep.tile([P, PACK, J], F32, name="down_rows")
+        for first in range(0, J, HIDDEN_GROUP):
+            tokens = slice(first, first + HIDDEN_GROUP)
+            for t in range(PACK):
+                down = psum.tile([P, HIDDEN_GROUP], F32, name="down", tag="for_scalar")
+                nc.tensor.matmul_mx(
+                    out=down[:],
+                    lhsT=wd_codes[:, t, :].bitcast(FP4X4),
+                    lhsT_scale=wd_plane[:, t, :],
+                    rhs=h_codes[:, tokens].bitcast(FP8X4),
+                    rhs_scale=h_plane[:, tokens],
+                    start=True,
+                    stop=True,
+                )
+                nc.scalar.copy(down_rows[:, t, tokens], down[:])
+
+        result = keep.tile([P, PACK, J], F32, name="result")
+        out_rows = out_0.rearrange("(p t) j -> p t j", t=PACK)
+
+        def add_residual(t, first, width):
+            tokens = slice(first, first + width)
+            nc.vector.tensor_tensor(
+                result[:, t, tokens],
+                residual[t][:].indirect(list_slice(first, width)),
+                down_rows[:, t, tokens],
+                ALU.add,
+            )
+            nc.sync.dma_start(out=out_rows[:, t, tokens], in_=result[:, t, tokens])
+
+        for first in range(0, J, HIDDEN_GROUP):
+            for t in range(PACK - 1):
+                add_residual(t, first, HIDDEN_GROUP)
+
+        rounded = []
+        for first in range(0, J, GROUP):
+            add_residual(PACK - 1, first, GROUP)
+            woven = keep.tile([P, GROUP * PACK], BF16, name="out_rounded%d" % first, align_bytes=64)
+            copy = nc.vector.tensor_copy if first == J - GROUP else nc.scalar.copy
+            copy(
+                woven[:].rearrange("p (c i t) -> p c t i", i=4, t=PACK),
+                result[:, :, first : first + GROUP].rearrange("p t (c i) -> p c t i", i=4),
+            )
+            rounded.append(woven)
 
         out_plane = keep.tile([P, J], U8, name="out_plane", align_bytes=64)
-        out_rows = out_0.rearrange("(p t) j -> p t j", t=PACK)
         out_words = out_1[0].rearrange("p j i -> p (j i)").bitcast(I32)
-        first = 0
-        for width in OUT_WIDTHS:
-            if first % GROUP == 0:
-                nc.vector.tensor_copy(
-                    picked_residual[:, PACK - 1, first : first + GROUP],
-                    residual[PACK - 1][:].indirect(list_slice(first, GROUP)),
-                )
-            result = keep.tile([P, PACK, width], F32, name="result%d" % first)
-            rounded = keep.tile([P, width * PACK], BF16, name="out_rounded%d" % first, align_bytes=64)
-            codes = keep.tile([P, width], I32, name="out_codes%d" % first, align_bytes=64)
-            for c in range(width // CHUNK):
-                cols = slice(c * CHUNK, (c + 1) * CHUNK)
-                tokens = slice(first + c * CHUNK, first + (c + 1) * CHUNK)
-                down = psum_out.tile([P, PACK, CHUNK], F32, name="down")
-                four_slices(
-                    down,
-                    lambda t: wd_codes[:, t, :].bitcast(FP4X4),
-                    lambda t: wd_plane[:, t, :],
-                    h_codes[:, tokens].bitcast(FP8X4),
-                    h_plane[:, tokens],
-                )
-                nc.vector.tensor_tensor(
-                    out=result[:, :, cols], in0=down[:], in1=picked_residual[:, :, tokens], op=ALU.add
-                )
-                nc.scalar.copy(
-                    rounded[:, c * CHUNK * PACK : (c + 1) * CHUNK * PACK].rearrange(
-                        "p (c i t) -> p c t i", i=4, t=PACK
-                    ),
-                    result[:, :, cols].rearrange("p t (c i) -> p c t i", i=4),
-                )
-            tokens = slice(first, first + width)
-            nc.sync.dma_start(out=out_rows[:, :, tokens], in_=result[:])
+        for g in (0, 1, 3, 2):
+            tokens = slice(g * GROUP, (g + 1) * GROUP)
+            codes = keep.tile([P, GROUP], I32, name="out_codes%d" % g, align_bytes=64)
             nc.vector.quantize_mx(
-                out=codes[:].bitcast(FP8X4), scales=out_plane[:, tokens], in_=rounded[:]
+                out=codes[:].bitcast(FP8X4), scales=out_plane[:, tokens], in_=rounded[g][:]
             )
             nc.sync.dma_start(out=out_words[:, tokens], in_=codes[:])
-            first = first + width
         for q in range(4):
             queue = nc.scalar if q % 2 == 0 else nc.sync
             queue.dma_start(

@@ -18,15 +18,19 @@ ALU = mybir.AluOpType
 P = 128
 PACK = 4
 CHUNK = 128
-GROUP = 256
 LIST_ROWS = 16
-SCALAR_SHARE = 64
-HIDDEN_GROUP = 512
+HALF = 512
+M_HALF = 64
+TABLE_LEAD = 256
+WORD_PIECES = (256, 256, 512)
+OUT_GROUPS = (512, 256, 128, 128)
+PLANE_GROUPS = (512, 256, 128, 128)
+LAG = 2
 
 
-def load_scale_rows(queue, plane, rows):
+def load_scale_rows(queues, plane, rows):
     for q in range(4):
-        queue.dma_start(
+        queues[q % len(queues)].dma_start(
             out=plane[32 * q : 32 * q + 4, :].bitcast(I32),
             in_=rows[4 * q : 4 * q + 4, :].bitcast(I32),
         )
@@ -38,15 +42,19 @@ def tile_list_gmlpt_relu_resLP_kernel(
     nc = tc.nc
     with ExitStack() as ctx:
         keep = ctx.enter_context(tc.tile_pool(name="keep", bufs=1))
-        ring = ctx.enter_context(tc.tile_pool(name="ring", bufs=4))
-        psum = ctx.enter_context(tc.psum_pool(name="psum", bufs=4))
+        ring = ctx.enter_context(tc.tile_pool(name="ring", bufs=2))
+        psum = ctx.enter_context(tc.psum_pool(name="psum", bufs=1))
 
         offsets = keep.tile([P, J // LIST_ROWS], U16, name="offsets")
         table_words = keep.tile([P, T], I32, name="table_words", align_bytes=64)
         table_plane = keep.tile([P, T], U8, name="table_plane", align_bytes=64)
-        wg_raw = keep.tile([P, PACK, R], F32, name="wg_raw")
-        wu_raw = keep.tile([P, PACK, R], F32, name="wu_raw")
-        wd_raw = keep.tile([P, 2 * N], U8, name="wd_raw")
+        wg_raw = [keep.tile([P, PACK, R // 2], F32, name="wg_raw%d" % a)[:] for a in range(2)]
+        staging = keep.tile([P, PACK * J], F32, name="staging")
+        wu_raw = [
+            staging[:, a * 2 * R : (a + 1) * 2 * R].rearrange("p (i r) -> p i r", i=PACK)
+            for a in range(2)
+        ]
+        wd_raw = keep.tile([P, 2 * N], U8, name="wd_raw", align_bytes=64)
         wd_plane_raw = keep.tile([P, N], U8, name="wd_plane_raw")
         residual = [keep.tile([P, T], F32, name="residual%d" % t) for t in range(PACK)]
 
@@ -54,110 +62,120 @@ def tile_list_gmlpt_relu_resLP_kernel(
         nc.gpsimd.memset(wd_plane_raw[:].bitcast(I32), 0)
 
         nc.sync.dma_start(offsets[:], offs)
+        table_rows = tab_words[0].rearrange("p t i -> p (t i)").bitcast(I32)
+        for a in range(2):
+            piece = slice(a * TABLE_LEAD, (a + 1) * TABLE_LEAD)
+            nc.sync.dma_start(out=table_words[:, piece], in_=table_rows[:, piece])
+        load_scale_rows((nc.sync, nc.scalar), table_plane, tab_scales[0])
+
+        def load_weight(raw, w):
+            rows = w.rearrange("(p i) r -> p i r", i=PACK)
+            for a in range(2):
+                nc.sync.dma_start(out=raw[a], in_=rows[:, :, a * (R // 2) : (a + 1) * (R // 2)])
+
+        load_weight(wg_raw, wg)
+        nc.sync.dma_start(out=table_words[:, 2 * TABLE_LEAD :], in_=table_rows[:, 2 * TABLE_LEAD :])
+        load_weight(wu_raw, wu)
         nc.sync.dma_start(out=wd_raw[:].bitcast(I32), in_=wd_words[0].bitcast(I32))
-        nc.sync.dma_start(
-            out=table_words[:], in_=tab_words[0].rearrange("p t i -> p (t i)").bitcast(I32)
-        )
-        load_scale_rows(nc.sync, table_plane, tab_scales[0])
-        nc.sync.dma_start(out=wg_raw[:], in_=wg.rearrange("(p i) r -> p i r", i=PACK))
-        nc.sync.dma_start(out=wu_raw[:], in_=wu.rearrange("(p i) r -> p i r", i=PACK))
-        load_scale_rows(nc.sync, wd_plane_raw, wd_scales[0])
+        load_scale_rows((nc.sync,), wd_plane_raw, wd_scales[0])
         residual_rows = rT.rearrange("(p t) c -> p t c", t=PACK)
         for t in range(PACK):
             nc.sync.dma_start(out=residual[t][:], in_=residual_rows[:, t, :])
 
-        wd_codes = keep.tile([P, PACK, 2 * P], U8, name="wd_codes", align_bytes=64)
-        nc.vector.tensor_copy(
-            wd_codes[:].rearrange("p t (m b) -> p m t b", b=2),
-            wd_raw[:].rearrange("p (m t b) -> p m t b", t=PACK, b=2),
-        )
-        picked_words = keep.tile([P, J], U32, name="picked_words", align_bytes=64)
-        nc.vector.tensor_copy(picked_words[:], table_words[:].bitcast(U32).indirect(offsets[:]))
+        def list_slice(first, count):
+            return offsets[:, first // LIST_ROWS : (first + count) // LIST_ROWS]
+
         picked_plane = keep.tile([P, J], U8, name="picked_plane", align_bytes=64)
         nc.vector.tensor_copy(picked_plane[:], table_plane[:].indirect(offsets[:]))
+        picked_words = keep.tile([P, J], U32, name="picked_words", align_bytes=64)
 
-        def quantise_weight(raw, name, scalar_columns):
-            rounded = keep.tile([P, PACK * R], BF16, name=name + "_rounded", align_bytes=64)
+        def round_columns(copy, rounded, raw, a, first, last):
+            dealt = rounded[:].rearrange("p (t m i) -> p m i t", t=PACK, i=PACK)
+            source = raw[a].rearrange("p i (m t) -> p m i t", t=PACK)
+            copy(dealt[:, a * M_HALF + first : a * M_HALF + last], source[:, first:last])
+
+        def quantise_weight(rounded, name):
             codes = keep.tile([P, R], U32, name=name + "_codes", align_bytes=64)
             plane = keep.tile([P, R], U8, name=name + "_plane", align_bytes=64)
-            dealt = rounded[:].rearrange("p (t m i) -> p m i t", t=PACK, i=PACK)
-            source = raw[:].rearrange("p i (m t) -> p m i t", t=PACK)
-            nc.scalar.copy(dealt[:, :scalar_columns], source[:, :scalar_columns])
-            if scalar_columns < P:
-                nc.vector.tensor_copy(dealt[:, scalar_columns:], source[:, scalar_columns:])
             nc.vector.quantize_mx(out=codes[:].bitcast(FP8X4), scales=plane[:], in_=rounded[:])
             return codes, plane
 
-        wg_codes, wg_plane = quantise_weight(wg_raw, "wg", P)
-        wu_codes, wu_plane = quantise_weight(wu_raw, "wu", SCALAR_SHARE)
+        wg_rounded = keep.tile([P, PACK * R], BF16, name="wg_rounded", align_bytes=64)
+        wu_rounded = keep.tile([P, PACK * R], BF16, name="wu_rounded", align_bytes=64)
+        round_columns(nc.scalar.copy, wg_rounded, wg_raw, 0, 0, M_HALF)
+        round_columns(nc.vector.tensor_copy, wg_rounded, wg_raw, 1, 0, M_HALF)
+        wg_codes, wg_plane = quantise_weight(wg_rounded, "wg")
+        first = 0
+        for width in WORD_PIECES:
+            nc.vector.tensor_copy(
+                picked_words[:, first : first + width],
+                table_words[:].bitcast(U32).indirect(list_slice(first, width)),
+            )
+            first = first + width
+        round_columns(nc.scalar.copy, wu_rounded, wu_raw, 0, 0, M_HALF)
+        round_columns(nc.vector.tensor_copy, wu_rounded, wu_raw, 1, 0, M_HALF)
+        wu_codes, wu_plane = quantise_weight(wu_rounded, "wu")
 
+        wd_codes = keep.tile([P, PACK, 2 * P], U8, name="wd_codes", tag="wu_rounded", align_bytes=64)
+        nc.vector.tensor_copy(
+            wd_codes[:].bitcast(U16).rearrange("p t m -> p m t"),
+            wd_raw[:].bitcast(U16).rearrange("p (m t) -> p m t", t=PACK),
+        )
         wd_plane = keep.tile([P, PACK, P], U8, name="wd_plane", align_bytes=64)
         nc.vector.tensor_copy(
             wd_plane[:].rearrange("p t m -> p m t"),
             wd_plane_raw[:].rearrange("p (m t) -> p m t", t=PACK),
         )
 
-        def list_slice(first, count):
-            return offsets[:, first // LIST_ROWS : (first + count) // LIST_ROWS]
-
-        def four_slices(bank, codes_of, plane_of, moving, moving_plane):
+        def first_product(tag, codes, plane, tokens):
+            bank = psum.tile([P, PACK, CHUNK], F32, name=tag, tag=tag)
             for t in range(PACK):
                 nc.tensor.matmul_mx(
                     out=bank[:, t, :],
-                    lhsT=codes_of(t),
-                    lhsT_scale=plane_of(t),
-                    rhs=moving,
-                    rhs_scale=moving_plane,
+                    lhsT=codes[:, t * P : (t + 1) * P].bitcast(FP8X4),
+                    lhsT_scale=plane[:, t * P : (t + 1) * P],
+                    rhs=picked_words[:, tokens].bitcast(FP8X4),
+                    rhs_scale=picked_plane[:, tokens],
                     start=True,
                     stop=True,
                 )
+            return bank
 
+        gate_woven = staging[:].rearrange("p (j t) -> p j t", t=PACK)
         h_codes = keep.tile([P, J], U32, name="h_codes", align_bytes=64)
         h_plane = keep.tile([P, J], U8, name="h_plane", align_bytes=64)
-        for first in range(0, J, HIDDEN_GROUP):
-            h_rounded = ring.tile([P, HIDDEN_GROUP * PACK], BF16, name="h_rounded", align_bytes=64)
-            for c in range(HIDDEN_GROUP // CHUNK):
+        chunks = HALF // CHUNK
+        for half in range(J // HALF):
+            first = half * HALF
+            for c in range(chunks):
                 tokens = slice(first + c * CHUNK, first + (c + 1) * CHUNK)
-                moving = picked_words[:, tokens].bitcast(FP8X4)
-                moving_plane = picked_plane[:, tokens]
-                gate = psum.tile([P, PACK, CHUNK], F32, name="gate", tag="for_scalar")
-                four_slices(
-                    gate,
-                    lambda t: wg_codes[:, t * P : (t + 1) * P].bitcast(FP8X4),
-                    lambda t: wg_plane[:, t * P : (t + 1) * P],
-                    moving,
-                    moving_plane,
-                )
-                up = psum.tile([P, PACK, CHUNK], F32, name="up", tag="for_vector")
-                four_slices(
-                    up,
-                    lambda t: wu_codes[:, t * P : (t + 1) * P].bitcast(FP8X4),
-                    lambda t: wu_plane[:, t * P : (t + 1) * P],
-                    moving,
-                    moving_plane,
-                )
-                gate_woven = ring.tile([P, CHUNK, PACK], F32, name="gate_woven")
-                nc.scalar.copy(gate_woven[:], gate[:].rearrange("p t j -> p j t"))
+                gate = first_product("bank%d" % (half * chunks + c), wg_codes, wg_plane, tokens)
+                nc.scalar.copy(gate_woven[:, tokens, :], gate[:].rearrange("p t j -> p j t"))
+            h_rounded = ring.tile([P, HALF * PACK], BF16, name="h_rounded", align_bytes=64)
+            for c in range(chunks):
+                tokens = slice(first + c * CHUNK, first + (c + 1) * CHUNK)
+                up = first_product("bank%d" % ((1 - half) * chunks + c), wu_codes, wu_plane, tokens)
                 nc.vector.scalar_tensor_tensor(
                     out=h_rounded[:, c * CHUNK * PACK : (c + 1) * CHUNK * PACK].rearrange(
                         "p (j t) -> p j t", t=PACK
                     ),
-                    in0=gate_woven[:],
+                    in0=gate_woven[:, tokens, :],
                     scalar=0.0,
                     in1=up[:].rearrange("p t j -> p j t"),
                     op0=ALU.max,
                     op1=ALU.mult,
                 )
-            tokens = slice(first, first + HIDDEN_GROUP)
+            tokens = slice(first, first + HALF)
             nc.vector.quantize_mx(
                 out=h_codes[:, tokens].bitcast(FP8X4), scales=h_plane[:, tokens], in_=h_rounded[:]
             )
 
-        down_rows = keep.tile([P, PACK, J], F32, name="down_rows")
-        for first in range(0, J, HIDDEN_GROUP):
-            tokens = slice(first, first + HIDDEN_GROUP)
+        trail = keep.tile([P, (2 * PACK + LAG) * HALF], F32, name="trail")
+        slots = trail[:].rearrange("p (s j) -> p s j", j=HALF)
+        for half in range(J // HALF):
+            tokens = slice(half * HALF, (half + 1) * HALF)
             for t in range(PACK):
-                down = psum.tile([P, HIDDEN_GROUP], F32, name="down", tag="for_scalar")
+                down = psum.tile([P, HALF], F32, name="down", tag="bank%d" % ((1 - half) * PACK + t))
                 nc.tensor.matmul_mx(
                     out=down[:],
                     lhsT=wd_codes[:, t, :].bitcast(FP4X4),
@@ -167,45 +185,47 @@ def tile_list_gmlpt_relu_resLP_kernel(
                     start=True,
                     stop=True,
                 )
-                nc.scalar.copy(down_rows[:, t, tokens], down[:])
+                nc.scalar.copy(slots[:, half * PACK + t + LAG, :], down[:])
 
-        result = keep.tile([P, PACK, J], F32, name="result")
         out_rows = out_0.rearrange("(p t) j -> p t j", t=PACK)
-
-        def add_residual(t, first, width):
-            tokens = slice(first, first + width)
-            nc.vector.tensor_tensor(
-                result[:, t, tokens],
-                residual[t][:].indirect(list_slice(first, width)),
-                down_rows[:, t, tokens],
-                ALU.add,
-            )
-            nc.sync.dma_start(out=out_rows[:, t, tokens], in_=result[:, t, tokens])
-
-        for first in range(0, J, HIDDEN_GROUP):
-            for t in range(PACK - 1):
-                add_residual(t, first, HIDDEN_GROUP)
-
-        rounded = []
-        for first in range(0, J, GROUP):
-            add_residual(PACK - 1, first, GROUP)
-            woven = keep.tile([P, GROUP * PACK], BF16, name="out_rounded%d" % first, align_bytes=64)
-            copy = nc.vector.tensor_copy if first == J - GROUP else nc.scalar.copy
-            copy(
-                woven[:].rearrange("p (c i t) -> p c t i", i=4, t=PACK),
-                result[:, :, first : first + GROUP].rearrange("p t (c i) -> p c t i", i=4),
-            )
-            rounded.append(woven)
-
-        out_plane = keep.tile([P, J], U8, name="out_plane", align_bytes=64)
         out_words = out_1[0].rearrange("p j i -> p (j i)").bitcast(I32)
-        for g in (0, 1, 3, 2):
-            tokens = slice(g * GROUP, (g + 1) * GROUP)
-            codes = keep.tile([P, GROUP], I32, name="out_codes%d" % g, align_bytes=64)
+        out_plane = keep.tile([P, J], U8, name="out_plane", align_bytes=64)
+        woven = keep.tile([P, PACK * J], BF16, name="woven", align_bytes=64)
+        first = 0
+        for width in OUT_GROUPS:
+            tokens = slice(first, first + width)
+            half, inside = divmod(first, HALF)
+            sums = slots[:, half * PACK : (half + 1) * PACK, inside : inside + width]
+            for t in range(PACK):
+                nc.vector.tensor_tensor(
+                    sums[:, t, :],
+                    residual[t][:].indirect(list_slice(first, width)),
+                    slots[:, half * PACK + t + LAG, inside : inside + width],
+                    ALU.add,
+                )
+                if width > CHUNK:
+                    nc.sync.dma_start(out=out_rows[:, t, tokens], in_=sums[:, t, :])
+            if width == CHUNK:
+                nc.sync.dma_start(out=out_rows[:, :, tokens], in_=sums)
+            nc.scalar.copy(
+                woven[:, PACK * first : PACK * (first + width)].rearrange(
+                    "p (c i t) -> p c t i", i=4, t=PACK
+                ),
+                sums.rearrange("p t (c i) -> p c t i", i=4),
+            )
+            first = first + width
+
+        first = 0
+        for width in PLANE_GROUPS:
+            tokens = slice(first, first + width)
+            codes = keep.tile([P, width], I32, name="out_codes%d" % first, align_bytes=64)
             nc.vector.quantize_mx(
-                out=codes[:].bitcast(FP8X4), scales=out_plane[:, tokens], in_=rounded[g][:]
+                out=codes[:].bitcast(FP8X4),
+                scales=out_plane[:, tokens],
+                in_=woven[:, PACK * first : PACK * (first + width)],
             )
             nc.sync.dma_start(out=out_words[:, tokens], in_=codes[:])
+            first = first + width
         for q in range(4):
             queue = nc.scalar if q % 2 == 0 else nc.sync
             queue.dma_start(

@@ -14,6 +14,7 @@ U8 = mybir.dt.uint8
 FP8X4 = mybir.dt.float8_e4m3fn_x4
 FP4X4 = mybir.dt.float4_e2m1fn_x4
 ALU = mybir.AluOpType
+ACT = mybir.ActivationFunctionType
 
 P = 128
 PACK = 4
@@ -26,6 +27,8 @@ WORD_PIECES = (256, 256, 512)
 OUT_GROUPS = (512, 256, 128, 128)
 PLANE_GROUPS = (512, 256, 128, 128)
 LAG = 2
+POOL_PIECE = 64
+DOWN_BANKS = (0, 1, 2, 3, 4, 6, 5, 7)
 
 
 def load_scale_rows(queues, plane, rows):
@@ -42,7 +45,6 @@ def tile_list_gmlpt_relu_resLP_kernel(
     nc = tc.nc
     with ExitStack() as ctx:
         keep = ctx.enter_context(tc.tile_pool(name="keep", bufs=1))
-        ring = ctx.enter_context(tc.tile_pool(name="ring", bufs=2))
         psum = ctx.enter_context(tc.psum_pool(name="psum", bufs=1))
 
         offsets = keep.tile([P, J // LIST_ROWS], U16, name="offsets")
@@ -141,41 +143,77 @@ def tile_list_gmlpt_relu_resLP_kernel(
                 )
             return bank
 
-        gate_woven = staging[:].rearrange("p (j t) -> p j t", t=PACK)
+        gate_slots = staging[:].rearrange("p (s j t) -> p s j t", j=CHUNK, t=PACK)
+        up_woven = keep.tile([P, 2, CHUNK, PACK], F32, name="up_woven")
+        h_rounded = keep.tile([P, J * PACK], BF16, name="h_rounded", align_bytes=64)
+        h_woven = h_rounded[:].rearrange("p (j t) -> p j t", t=PACK)
         h_codes = keep.tile([P, J], U32, name="h_codes", align_bytes=64)
         h_plane = keep.tile([P, J], U8, name="h_plane", align_bytes=64)
-        chunks = HALF // CHUNK
-        for half in range(J // HALF):
-            first = half * HALF
-            for c in range(chunks):
-                tokens = slice(first + c * CHUNK, first + (c + 1) * CHUNK)
-                gate = first_product("bank%d" % (half * chunks + c), wg_codes, wg_plane, tokens)
-                nc.scalar.copy(gate_woven[:, tokens, :], gate[:].rearrange("p t j -> p j t"))
-            h_rounded = ring.tile([P, HALF * PACK], BF16, name="h_rounded", align_bytes=64)
-            for c in range(chunks):
-                tokens = slice(first + c * CHUNK, first + (c + 1) * CHUNK)
-                up = first_product("bank%d" % ((1 - half) * chunks + c), wu_codes, wu_plane, tokens)
-                nc.vector.scalar_tensor_tensor(
-                    out=h_rounded[:, c * CHUNK * PACK : (c + 1) * CHUNK * PACK].rearrange(
-                        "p (j t) -> p j t", t=PACK
-                    ),
-                    in0=gate_woven[:, tokens, :],
-                    scalar=0.0,
-                    in1=up[:].rearrange("p t j -> p j t"),
-                    op0=ALU.max,
-                    op1=ALU.mult,
-                )
-            tokens = slice(first, first + HALF)
-            nc.vector.quantize_mx(
-                out=h_codes[:, tokens].bitcast(FP8X4), scales=h_plane[:, tokens], in_=h_rounded[:]
+        slot_of = {}
+
+        def chunk(c):
+            return slice(c * CHUNK, (c + 1) * CHUNK)
+
+        def gate(c, bank):
+            slot_of.setdefault(c, len(slot_of))
+            product = first_product("bank%d" % bank, wg_codes, wg_plane, chunk(c))
+            nc.scalar.activation(
+                gate_slots[:, slot_of[c]], product[:].rearrange("p t j -> p j t"), ACT.Relu
             )
+
+        def hidden_on_vector(c, bank):
+            up = first_product("bank%d" % bank, wu_codes, wu_plane, chunk(c))
+            nc.vector.tensor_tensor(
+                h_woven[:, chunk(c), :],
+                gate_slots[:, slot_of[c]],
+                up[:].rearrange("p t j -> p j t"),
+                ALU.mult,
+            )
+
+        def hidden_on_gpsimd(c, bank):
+            up = first_product("bank%d" % bank, wu_codes, wu_plane, chunk(c))
+            nc.scalar.copy(up_woven[:, c % 2], up[:].rearrange("p t j -> p j t"))
+            for a in range(0, CHUNK, POOL_PIECE):
+                nc.gpsimd.tensor_tensor(
+                    h_woven[:, c * CHUNK + a : c * CHUNK + a + POOL_PIECE, :],
+                    gate_slots[:, slot_of[c], a : a + POOL_PIECE, :],
+                    up_woven[:, c % 2, a : a + POOL_PIECE, :],
+                    ALU.mult,
+                )
+
+        def quantise_hidden(half):
+            tokens = slice(half * HALF, (half + 1) * HALF)
+            nc.vector.quantize_mx(
+                out=h_codes[:, tokens].bitcast(FP8X4),
+                scales=h_plane[:, tokens],
+                in_=h_rounded[:, half * HALF * PACK : (half + 1) * HALF * PACK],
+            )
+
+        gate(0, 0)
+        gate(1, 1)
+        gate(6, 2)
+        gate(7, 3)
+        hidden_on_vector(0, 4)
+        gate(2, 0)
+        hidden_on_gpsimd(6, 5)
+        hidden_on_vector(1, 6)
+        gate(3, 1)
+        hidden_on_gpsimd(7, 7)
+        hidden_on_vector(2, 2)
+        gate(4, 4)
+        hidden_on_vector(3, 3)
+        gate(5, 6)
+        quantise_hidden(0)
+        hidden_on_vector(4, 5)
+        hidden_on_vector(5, 7)
+        quantise_hidden(1)
 
         trail = keep.tile([P, (2 * PACK + LAG) * HALF], F32, name="trail")
         slots = trail[:].rearrange("p (s j) -> p s j", j=HALF)
         for half in range(J // HALF):
             tokens = slice(half * HALF, (half + 1) * HALF)
             for t in range(PACK):
-                down = psum.tile([P, HALF], F32, name="down", tag="bank%d" % ((1 - half) * PACK + t))
+                down = psum.tile([P, HALF], F32, name="down", tag="bank%d" % DOWN_BANKS[half * PACK + t])
                 nc.tensor.matmul_mx(
                     out=down[:],
                     lhsT=wd_codes[:, t, :].bitcast(FP4X4),

@@ -25,8 +25,7 @@ M_HALF = 64
 TABLE_LEAD = 256
 WORD_PIECES = (256, 256, 512)
 OUT_GROUPS = (512, 256, 128, 128)
-PLANE_GROUPS = (512, 256, 128, 128)
-LAG = 2
+WORD_STORE_ENDS = (512, 896, 1024)
 POOL_PIECE = 64
 DOWN_BANKS = (0, 1, 2, 3, 4, 6, 5, 7)
 
@@ -208,22 +207,29 @@ def tile_list_gmlpt_relu_resLP_kernel(
         hidden_on_vector(5, 7)
         quantise_hidden(1)
 
-        trail = keep.tile([P, (2 * PACK + LAG) * HALF], F32, name="trail")
-        slots = trail[:].rearrange("p (s j) -> p s j", j=HALF)
-        for half in range(J // HALF):
-            tokens = slice(half * HALF, (half + 1) * HALF)
-            for t in range(PACK):
-                down = psum.tile([P, HALF], F32, name="down", tag="bank%d" % DOWN_BANKS[half * PACK + t])
-                nc.tensor.matmul_mx(
-                    out=down[:],
-                    lhsT=wd_codes[:, t, :].bitcast(FP4X4),
-                    lhsT_scale=wd_plane[:, t, :],
-                    rhs=h_codes[:, tokens].bitcast(FP8X4),
-                    rhs_scale=h_plane[:, tokens],
-                    start=True,
-                    stop=True,
-                )
-                nc.scalar.copy(slots[:, half * PACK + t + LAG, :], down[:])
+        trail = keep.tile([P, PACK * J], F32, name="trail")
+        first_sums = keep.tile([P, PACK * HALF], F32, name="first_sums")
+        first = 0
+        bank = 0
+        for width in OUT_GROUPS:
+            tokens = slice(first, first + width)
+            per_bank = HALF // width
+            for t0 in range(0, PACK, per_bank):
+                down = psum.tile([P, per_bank, width], F32, name="down", tag="bank%d" % DOWN_BANKS[bank])
+                bank = bank + 1
+                for u in range(per_bank):
+                    nc.tensor.matmul_mx(
+                        out=down[:, u, :],
+                        lhsT=wd_codes[:, t0 + u, :].bitcast(FP4X4),
+                        lhsT_scale=wd_plane[:, t0 + u, :],
+                        rhs=h_codes[:, tokens].bitcast(FP8X4),
+                        rhs_scale=h_plane[:, tokens],
+                        start=True,
+                        stop=True,
+                    )
+                at = PACK * first + t0 * width
+                nc.scalar.copy(trail[:, at : at + HALF], down[:].rearrange("p u j -> p (u j)"))
+            first = first + width
 
         out_rows = out_0.rearrange("(p t) j -> p t j", t=PACK)
         out_words = out_1[0].rearrange("p j i -> p (j i)").bitcast(I32)
@@ -232,19 +238,24 @@ def tile_list_gmlpt_relu_resLP_kernel(
         first = 0
         for width in OUT_GROUPS:
             tokens = slice(first, first + width)
-            half, inside = divmod(first, HALF)
-            sums = slots[:, half * PACK : (half + 1) * PACK, inside : inside + width]
+            base = PACK * first
+            if first == 0:
+                sums = first_sums[:]
+            else:
+                sums = trail[:, base - HALF : base - HALF + PACK * width]
+            sums = sums.rearrange("p (t j) -> p t j", t=PACK)
             for t in range(PACK):
                 nc.vector.tensor_tensor(
                     sums[:, t, :],
                     residual[t][:].indirect(list_slice(first, width)),
-                    slots[:, half * PACK + t + LAG, inside : inside + width],
+                    trail[:, base + t * width : base + (t + 1) * width],
                     ALU.add,
                 )
                 if width > CHUNK:
                     nc.sync.dma_start(out=out_rows[:, t, tokens], in_=sums[:, t, :])
-            if width == CHUNK:
-                nc.sync.dma_start(out=out_rows[:, :, tokens], in_=sums)
+                elif t % 2 == 1:
+                    pair = slice(t - 1, t + 1)
+                    nc.sync.dma_start(out=out_rows[:, pair, tokens], in_=sums[:, pair, :])
             nc.scalar.copy(
                 woven[:, PACK * first : PACK * (first + width)].rearrange(
                     "p (c i t) -> p c t i", i=4, t=PACK
@@ -253,17 +264,20 @@ def tile_list_gmlpt_relu_resLP_kernel(
             )
             first = first + width
 
+        out_codes = keep.tile([P, J], I32, name="out_codes", align_bytes=64)
         first = 0
-        for width in PLANE_GROUPS:
+        stored = 0
+        for width in OUT_GROUPS:
             tokens = slice(first, first + width)
-            codes = keep.tile([P, width], I32, name="out_codes%d" % first, align_bytes=64)
             nc.vector.quantize_mx(
-                out=codes[:].bitcast(FP8X4),
+                out=out_codes[:, tokens].bitcast(FP8X4),
                 scales=out_plane[:, tokens],
                 in_=woven[:, PACK * first : PACK * (first + width)],
             )
-            nc.sync.dma_start(out=out_words[:, tokens], in_=codes[:])
             first = first + width
+            if first in WORD_STORE_ENDS:
+                nc.sync.dma_start(out=out_words[:, stored:first], in_=out_codes[:, stored:first])
+                stored = first
         for q in range(4):
             queue = nc.scalar if q % 2 == 0 else nc.sync
             queue.dma_start(

@@ -23,10 +23,10 @@ LIST_ROWS = 16
 HALF = 512
 M_HALF = 64
 TABLE_LEAD = 256
-WORD_PIECES = (256, 256, 512)
-OUT_GROUPS = (512, 256, 128, 128)
+OUT_GROUPS = (512, 256, 256)
+PLANE_GROUPS = (512, 256, 128, 128)
 WORD_STORE_ENDS = (512, 896, 1024)
-POOL_PIECE = 64
+WG_SCALAR_COLUMNS = 40
 DOWN_BANKS = (0, 1, 2, 3, 4, 6, 5, 7)
 
 
@@ -88,7 +88,15 @@ def tile_list_gmlpt_relu_resLP_kernel(
 
         picked_plane = keep.tile([P, J], U8, name="picked_plane", align_bytes=64)
         nc.vector.tensor_copy(picked_plane[:], table_plane[:].indirect(offsets[:]))
-        picked_words = keep.tile([P, J], U32, name="picked_words", align_bytes=64)
+        picked_words = {}
+
+        def gather_words(tile, tile_first, first, width):
+            piece = tile[:, first - tile_first : first - tile_first + width]
+            nc.vector.tensor_copy(
+                piece, table_words[:].bitcast(U32).indirect(list_slice(first, width))
+            )
+            for a in range(0, width, CHUNK):
+                picked_words.setdefault(first + a, piece[:, a : a + CHUNK])
 
         def round_columns(copy, rounded, raw, a, first, last):
             dealt = rounded[:].rearrange("p (t m i) -> p m i t", t=PACK, i=PACK)
@@ -104,20 +112,19 @@ def tile_list_gmlpt_relu_resLP_kernel(
         wg_rounded = keep.tile([P, PACK * R], BF16, name="wg_rounded", align_bytes=64)
         wu_rounded = keep.tile([P, PACK * R], BF16, name="wu_rounded", align_bytes=64)
         round_columns(nc.scalar.copy, wg_rounded, wg_raw, 0, 0, M_HALF)
-        round_columns(nc.vector.tensor_copy, wg_rounded, wg_raw, 1, 0, M_HALF)
+        round_columns(nc.scalar.copy, wg_rounded, wg_raw, 1, 0, WG_SCALAR_COLUMNS)
+        round_columns(nc.vector.tensor_copy, wg_rounded, wg_raw, 1, WG_SCALAR_COLUMNS, M_HALF)
         wg_codes, wg_plane = quantise_weight(wg_rounded, "wg")
-        first = 0
-        for width in WORD_PIECES:
-            nc.vector.tensor_copy(
-                picked_words[:, first : first + width],
-                table_words[:].bitcast(U32).indirect(list_slice(first, width)),
-            )
-            first = first + width
+        early = keep.tile([P, 768], U32, name="picked_early", tag="wg_rounded", align_bytes=64)
+        gather_words(early, 0, 0, 256)
+        gather_words(early, 0, 256, 512)
         round_columns(nc.scalar.copy, wu_rounded, wu_raw, 0, 0, M_HALF)
         round_columns(nc.vector.tensor_copy, wu_rounded, wu_raw, 1, 0, M_HALF)
         wu_codes, wu_plane = quantise_weight(wu_rounded, "wu")
+        late = keep.tile([P, 256], U32, name="picked_late", tag="wu_rounded", align_bytes=64)
+        gather_words(late, 768, 768, 256)
 
-        wd_codes = keep.tile([P, PACK, 2 * P], U8, name="wd_codes", tag="wu_rounded", align_bytes=64)
+        wd_codes = keep.tile([P, PACK, 2 * P], U8, name="wd_codes", align_bytes=64)
         nc.vector.tensor_copy(
             wd_codes[:].bitcast(U16).rearrange("p t m -> p m t"),
             wd_raw[:].bitcast(U16).rearrange("p (m t) -> p m t", t=PACK),
@@ -135,7 +142,7 @@ def tile_list_gmlpt_relu_resLP_kernel(
                     out=bank[:, t, :],
                     lhsT=codes[:, t * P : (t + 1) * P].bitcast(FP8X4),
                     lhsT_scale=plane[:, t * P : (t + 1) * P],
-                    rhs=picked_words[:, tokens].bitcast(FP8X4),
+                    rhs=picked_words[tokens.start].bitcast(FP8X4),
                     rhs_scale=picked_plane[:, tokens],
                     start=True,
                     stop=True,
@@ -169,14 +176,14 @@ def tile_list_gmlpt_relu_resLP_kernel(
                 ALU.mult,
             )
 
-        def hidden_on_gpsimd(c, bank):
+        def hidden_on_gpsimd(c, bank, piece):
             up = first_product("bank%d" % bank, wu_codes, wu_plane, chunk(c))
             nc.scalar.copy(up_woven[:, c % 2], up[:].rearrange("p t j -> p j t"))
-            for a in range(0, CHUNK, POOL_PIECE):
+            for a in range(0, CHUNK, piece):
                 nc.gpsimd.tensor_tensor(
-                    h_woven[:, c * CHUNK + a : c * CHUNK + a + POOL_PIECE, :],
-                    gate_slots[:, slot_of[c], a : a + POOL_PIECE, :],
-                    up_woven[:, c % 2, a : a + POOL_PIECE, :],
+                    h_woven[:, c * CHUNK + a : c * CHUNK + a + piece, :],
+                    gate_slots[:, slot_of[c], a : a + piece, :],
+                    up_woven[:, c % 2, a : a + piece, :],
                     ALU.mult,
                 )
 
@@ -190,21 +197,21 @@ def tile_list_gmlpt_relu_resLP_kernel(
 
         gate(0, 0)
         gate(1, 1)
-        gate(6, 2)
-        gate(7, 3)
+        gate(4, 2)
+        gate(2, 3)
         hidden_on_vector(0, 4)
-        gate(2, 0)
-        hidden_on_gpsimd(6, 5)
+        hidden_on_gpsimd(4, 5, 128)
+        gate(3, 0)
         hidden_on_vector(1, 6)
-        gate(3, 1)
-        hidden_on_gpsimd(7, 7)
+        gate(5, 1)
+        hidden_on_gpsimd(5, 7, 32)
         hidden_on_vector(2, 2)
-        gate(4, 4)
+        gate(6, 4)
         hidden_on_vector(3, 3)
-        gate(5, 6)
+        gate(7, 6)
         quantise_hidden(0)
-        hidden_on_vector(4, 5)
-        hidden_on_vector(5, 7)
+        hidden_on_vector(6, 5)
+        hidden_on_vector(7, 7)
         quantise_hidden(1)
 
         trail = keep.tile([P, PACK * J], F32, name="trail")
@@ -244,30 +251,31 @@ def tile_list_gmlpt_relu_resLP_kernel(
             else:
                 sums = trail[:, base - HALF : base - HALF + PACK * width]
             sums = sums.rearrange("p (t j) -> p t j", t=PACK)
+            last = first + width == J
             for t in range(PACK):
-                nc.vector.tensor_tensor(
-                    sums[:, t, :],
-                    residual[t][:].indirect(list_slice(first, width)),
-                    trail[:, base + t * width : base + (t + 1) * width],
-                    ALU.add,
+                step = CHUNK if last and t == PACK - 1 else width
+                for a in range(0, width, step):
+                    nc.vector.tensor_tensor(
+                        sums[:, t, a : a + step],
+                        residual[t][:].indirect(list_slice(first + a, step)),
+                        trail[:, base + t * width + a : base + t * width + a + step],
+                        ALU.add,
+                    )
+                nc.sync.dma_start(out=out_rows[:, t, tokens], in_=sums[:, t, :])
+            step = CHUNK if last else width
+            for a in range(0, width, step):
+                nc.scalar.copy(
+                    woven[:, PACK * (first + a) : PACK * (first + a + step)].rearrange(
+                        "p (c i t) -> p c t i", i=4, t=PACK
+                    ),
+                    sums[:, :, a : a + step].rearrange("p t (c i) -> p c t i", i=4),
                 )
-                if width > CHUNK:
-                    nc.sync.dma_start(out=out_rows[:, t, tokens], in_=sums[:, t, :])
-                elif t % 2 == 1:
-                    pair = slice(t - 1, t + 1)
-                    nc.sync.dma_start(out=out_rows[:, pair, tokens], in_=sums[:, pair, :])
-            nc.scalar.copy(
-                woven[:, PACK * first : PACK * (first + width)].rearrange(
-                    "p (c i t) -> p c t i", i=4, t=PACK
-                ),
-                sums.rearrange("p t (c i) -> p c t i", i=4),
-            )
             first = first + width
 
         out_codes = keep.tile([P, J], I32, name="out_codes", align_bytes=64)
         first = 0
         stored = 0
-        for width in OUT_GROUPS:
+        for width in PLANE_GROUPS:
             tokens = slice(first, first + width)
             nc.vector.quantize_mx(
                 out=out_codes[:, tokens].bitcast(FP8X4),

@@ -25,7 +25,7 @@ M_HALF = 64
 TABLE_LEAD = 256
 OUT_GROUPS = (512, 256, 256)
 PLANE_GROUPS = (512, 256, 128, 128)
-WORD_STORE_ENDS = (512, 896, 1024)
+WORD_STORE_ENDS = (512, 768, 1024)
 WG_SCALAR_COLUMNS = 40
 DOWN_BANKS = (0, 1, 2, 3, 4, 6, 5, 7)
 
@@ -44,6 +44,7 @@ def tile_list_gmlpt_relu_resLP_kernel(
     nc = tc.nc
     with ExitStack() as ctx:
         keep = ctx.enter_context(tc.tile_pool(name="keep", bufs=1))
+        reuse = ctx.enter_context(tc.tile_pool(name="reuse", bufs=1))
         psum = ctx.enter_context(tc.psum_pool(name="psum", bufs=1))
 
         offsets = keep.tile([P, J // LIST_ROWS], U16, name="offsets")
@@ -110,7 +111,7 @@ def tile_list_gmlpt_relu_resLP_kernel(
             return codes, plane
 
         wg_rounded = keep.tile([P, PACK * R], BF16, name="wg_rounded", align_bytes=64)
-        wu_rounded = keep.tile([P, PACK * R], BF16, name="wu_rounded", align_bytes=64)
+        wu_rounded = reuse.tile([P, PACK * R], BF16, name="wu_rounded", offset=0, align_bytes=64)
         round_columns(nc.scalar.copy, wg_rounded, wg_raw, 0, 0, M_HALF)
         round_columns(nc.scalar.copy, wg_rounded, wg_raw, 1, 0, WG_SCALAR_COLUMNS)
         round_columns(nc.vector.tensor_copy, wg_rounded, wg_raw, 1, WG_SCALAR_COLUMNS, M_HALF)
@@ -121,7 +122,7 @@ def tile_list_gmlpt_relu_resLP_kernel(
         round_columns(nc.scalar.copy, wu_rounded, wu_raw, 0, 0, M_HALF)
         round_columns(nc.vector.tensor_copy, wu_rounded, wu_raw, 1, 0, M_HALF)
         wu_codes, wu_plane = quantise_weight(wu_rounded, "wu")
-        late = keep.tile([P, 256], U32, name="picked_late", tag="wu_rounded", align_bytes=64)
+        late = reuse.tile([P, 256], U32, name="picked_late", offset=0, align_bytes=64)
         gather_words(late, 768, 768, 256)
 
         wd_codes = keep.tile([P, PACK, 2 * P], U8, name="wd_codes", align_bytes=64)
@@ -129,7 +130,7 @@ def tile_list_gmlpt_relu_resLP_kernel(
             wd_codes[:].bitcast(U16).rearrange("p t m -> p m t"),
             wd_raw[:].bitcast(U16).rearrange("p (m t) -> p m t", t=PACK),
         )
-        wd_plane = keep.tile([P, PACK, P], U8, name="wd_plane", align_bytes=64)
+        wd_plane = reuse.tile([P, PACK, P], U8, name="wd_plane", offset=1024, align_bytes=64)
         nc.vector.tensor_copy(
             wd_plane[:].rearrange("p t m -> p m t"),
             wd_plane_raw[:].rearrange("p (m t) -> p m t", t=PACK),
@@ -151,8 +152,14 @@ def tile_list_gmlpt_relu_resLP_kernel(
 
         gate_slots = staging[:].rearrange("p (s j t) -> p s j t", j=CHUNK, t=PACK)
         up_woven = keep.tile([P, 2, CHUNK, PACK], F32, name="up_woven")
-        h_rounded = keep.tile([P, J * PACK], BF16, name="h_rounded", align_bytes=64)
-        h_woven = h_rounded[:].rearrange("p (j t) -> p j t", t=PACK)
+        h_rounded = keep.tile([P, (J - 2 * CHUNK) * PACK], BF16, name="h_rounded", align_bytes=64)
+        h_tokens = h_rounded[:].rearrange("p (j t) -> p j t", t=PACK)
+        h_halves = [h_tokens[:, HALF - 2 * CHUNK :, :], h_tokens[:, :HALF, :]]
+
+        def h_woven(first, count):
+            half, inside = divmod(first, HALF)
+            return h_halves[half][:, inside : inside + count, :]
+
         h_codes = keep.tile([P, J], U32, name="h_codes", align_bytes=64)
         h_plane = keep.tile([P, J], U8, name="h_plane", align_bytes=64)
         slot_of = {}
@@ -170,7 +177,7 @@ def tile_list_gmlpt_relu_resLP_kernel(
         def hidden_on_vector(c, bank):
             up = first_product("bank%d" % bank, wu_codes, wu_plane, chunk(c))
             nc.vector.tensor_tensor(
-                h_woven[:, chunk(c), :],
+                h_woven(c * CHUNK, CHUNK),
                 gate_slots[:, slot_of[c]],
                 up[:].rearrange("p t j -> p j t"),
                 ALU.mult,
@@ -178,12 +185,12 @@ def tile_list_gmlpt_relu_resLP_kernel(
 
         def hidden_on_gpsimd(c, bank, piece):
             up = first_product("bank%d" % bank, wu_codes, wu_plane, chunk(c))
-            nc.scalar.copy(up_woven[:, c % 2], up[:].rearrange("p t j -> p j t"))
+            nc.scalar.copy(up_woven[:, c // PACK], up[:].rearrange("p t j -> p j t"))
             for a in range(0, CHUNK, piece):
                 nc.gpsimd.tensor_tensor(
-                    h_woven[:, c * CHUNK + a : c * CHUNK + a + piece, :],
+                    h_woven(c * CHUNK + a, piece),
                     gate_slots[:, slot_of[c], a : a + piece, :],
-                    up_woven[:, c % 2, a : a + piece, :],
+                    up_woven[:, c // PACK, a : a + piece, :],
                     ALU.mult,
                 )
 
@@ -192,22 +199,22 @@ def tile_list_gmlpt_relu_resLP_kernel(
             nc.vector.quantize_mx(
                 out=h_codes[:, tokens].bitcast(FP8X4),
                 scales=h_plane[:, tokens],
-                in_=h_rounded[:, half * HALF * PACK : (half + 1) * HALF * PACK],
+                in_=h_halves[half].rearrange("p j t -> p (j t)"),
             )
 
         gate(0, 0)
         gate(1, 1)
-        gate(4, 2)
+        gate(3, 2)
         gate(2, 3)
         hidden_on_vector(0, 4)
-        hidden_on_gpsimd(4, 5, 128)
-        gate(3, 0)
+        hidden_on_gpsimd(3, 5, 128)
+        gate(4, 0)
         hidden_on_vector(1, 6)
         gate(5, 1)
         hidden_on_gpsimd(5, 7, 32)
         hidden_on_vector(2, 2)
         gate(6, 4)
-        hidden_on_vector(3, 3)
+        hidden_on_vector(4, 3)
         gate(7, 6)
         quantise_hidden(0)
         hidden_on_vector(6, 5)

@@ -18,16 +18,18 @@ ACT = mybir.ActivationFunctionType
 
 P = 128
 PACK = 4
-CHUNK = 128
 LIST_ROWS = 16
-HALF = 512
-M_HALF = 64
+BANK = 512
+CHUNK = BANK // PACK
+HALF = J // 2
+M_HALF = P // 2
 TABLE_LEAD = 256
+WG_SCALAR_COLUMNS = 40
+FIRST_WORDS, EARLY_WORDS = 256, 768
 OUT_GROUPS = (512, 256, 256)
+FIRST_Y_PIECE = 256
 PLANE_GROUPS = (512, 256, 128, 128)
 WORD_STORE_ENDS = (512, 768, 1024)
-WG_SCALAR_COLUMNS = 40
-DOWN_BANKS = (0, 1, 2, 3, 4, 6, 5, 7)
 
 
 def load_scale_rows(queues, plane, rows):
@@ -44,16 +46,16 @@ def tile_list_gmlpt_relu_resLP_kernel(
     nc = tc.nc
     with ExitStack() as ctx:
         keep = ctx.enter_context(tc.tile_pool(name="keep", bufs=1))
-        reuse = ctx.enter_context(tc.tile_pool(name="reuse", bufs=1))
+        after_wu = ctx.enter_context(tc.tile_pool(name="after_wu", bufs=1))
         psum = ctx.enter_context(tc.psum_pool(name="psum", bufs=1))
 
         offsets = keep.tile([P, J // LIST_ROWS], U16, name="offsets")
         table_words = keep.tile([P, T], I32, name="table_words", align_bytes=64)
         table_plane = keep.tile([P, T], U8, name="table_plane", align_bytes=64)
         wg_raw = [keep.tile([P, PACK, R // 2], F32, name="wg_raw%d" % a)[:] for a in range(2)]
-        staging = keep.tile([P, PACK * J], F32, name="staging")
+        wu_then_gates = keep.tile([P, PACK * J], F32, name="wu_then_gates")
         wu_raw = [
-            staging[:, a * 2 * R : (a + 1) * 2 * R].rearrange("p (i r) -> p i r", i=PACK)
+            wu_then_gates[:, a * 2 * R : (a + 1) * 2 * R].rearrange("p (i r) -> p i r", i=PACK)
             for a in range(2)
         ]
         wd_raw = keep.tile([P, 2 * N], U8, name="wd_raw", align_bytes=64)
@@ -66,8 +68,8 @@ def tile_list_gmlpt_relu_resLP_kernel(
         nc.sync.dma_start(offsets[:], offs)
         table_rows = tab_words[0].rearrange("p t i -> p (t i)").bitcast(I32)
         for a in range(2):
-            piece = slice(a * TABLE_LEAD, (a + 1) * TABLE_LEAD)
-            nc.sync.dma_start(out=table_words[:, piece], in_=table_rows[:, piece])
+            lead = slice(a * TABLE_LEAD, (a + 1) * TABLE_LEAD)
+            nc.sync.dma_start(out=table_words[:, lead], in_=table_rows[:, lead])
         load_scale_rows((nc.sync, nc.scalar), table_plane, tab_scales[0])
 
         def load_weight(raw, w):
@@ -89,15 +91,11 @@ def tile_list_gmlpt_relu_resLP_kernel(
 
         picked_plane = keep.tile([P, J], U8, name="picked_plane", align_bytes=64)
         nc.vector.tensor_copy(picked_plane[:], table_plane[:].indirect(offsets[:]))
-        picked_words = {}
 
-        def gather_words(tile, tile_first, first, width):
-            piece = tile[:, first - tile_first : first - tile_first + width]
+        def gather_words(picked, first, count):
             nc.vector.tensor_copy(
-                piece, table_words[:].bitcast(U32).indirect(list_slice(first, width))
+                picked, table_words[:].bitcast(U32).indirect(list_slice(first, count))
             )
-            for a in range(0, width, CHUNK):
-                picked_words.setdefault(first + a, piece[:, a : a + CHUNK])
 
         def round_columns(copy, rounded, raw, a, first, last):
             dealt = rounded[:].rearrange("p (t m i) -> p m i t", t=PACK, i=PACK)
@@ -111,88 +109,83 @@ def tile_list_gmlpt_relu_resLP_kernel(
             return codes, plane
 
         wg_rounded = keep.tile([P, PACK * R], BF16, name="wg_rounded", align_bytes=64)
-        wu_rounded = reuse.tile([P, PACK * R], BF16, name="wu_rounded", offset=0, align_bytes=64)
+        wu_rounded = after_wu.tile([P, PACK * R], BF16, name="wu_rounded", offset=0, align_bytes=64)
         round_columns(nc.scalar.copy, wg_rounded, wg_raw, 0, 0, M_HALF)
         round_columns(nc.scalar.copy, wg_rounded, wg_raw, 1, 0, WG_SCALAR_COLUMNS)
         round_columns(nc.vector.tensor_copy, wg_rounded, wg_raw, 1, WG_SCALAR_COLUMNS, M_HALF)
         wg_codes, wg_plane = quantise_weight(wg_rounded, "wg")
-        early = keep.tile([P, 768], U32, name="picked_early", tag="wg_rounded", align_bytes=64)
-        gather_words(early, 0, 0, 256)
-        gather_words(early, 0, 256, 512)
+        early_words = keep.tile(
+            [P, EARLY_WORDS], U32, name="early_words", tag="wg_rounded", align_bytes=64
+        )
+        gather_words(early_words[:, :FIRST_WORDS], 0, FIRST_WORDS)
+        gather_words(early_words[:, FIRST_WORDS:], FIRST_WORDS, EARLY_WORDS - FIRST_WORDS)
         round_columns(nc.scalar.copy, wu_rounded, wu_raw, 0, 0, M_HALF)
         round_columns(nc.vector.tensor_copy, wu_rounded, wu_raw, 1, 0, M_HALF)
         wu_codes, wu_plane = quantise_weight(wu_rounded, "wu")
-        late = reuse.tile([P, 256], U32, name="picked_late", offset=0, align_bytes=64)
-        gather_words(late, 768, 768, 256)
+        late_words = after_wu.tile(
+            [P, J - EARLY_WORDS], U32, name="late_words", offset=0, align_bytes=64
+        )
+        gather_words(late_words[:], EARLY_WORDS, J - EARLY_WORDS)
 
         wd_codes = keep.tile([P, PACK, 2 * P], U8, name="wd_codes", align_bytes=64)
         nc.vector.tensor_copy(
             wd_codes[:].bitcast(U16).rearrange("p t m -> p m t"),
             wd_raw[:].bitcast(U16).rearrange("p (m t) -> p m t", t=PACK),
         )
-        wd_plane = reuse.tile([P, PACK, P], U8, name="wd_plane", offset=1024, align_bytes=64)
+        wd_plane = after_wu.tile(
+            [P, PACK, P], U8, name="wd_plane", offset=4 * (J - EARLY_WORDS), align_bytes=64
+        )
         nc.vector.tensor_copy(
             wd_plane[:].rearrange("p t m -> p m t"),
             wd_plane_raw[:].rearrange("p (m t) -> p m t", t=PACK),
         )
 
-        def first_product(tag, codes, plane, tokens):
-            bank = psum.tile([P, PACK, CHUNK], F32, name=tag, tag=tag)
+        def first_product(bank, codes, plane, c):
+            first = c * CHUNK
+            if first < EARLY_WORDS:
+                words = early_words[:, first : first + CHUNK]
+            else:
+                words = late_words[:, first - EARLY_WORDS : first - EARLY_WORDS + CHUNK]
+            product = psum.tile([P, PACK, CHUNK], F32, name="product", tag="bank%d" % bank)
             for t in range(PACK):
                 nc.tensor.matmul_mx(
-                    out=bank[:, t, :],
+                    out=product[:, t, :],
                     lhsT=codes[:, t * P : (t + 1) * P].bitcast(FP8X4),
                     lhsT_scale=plane[:, t * P : (t + 1) * P],
-                    rhs=picked_words[tokens.start].bitcast(FP8X4),
-                    rhs_scale=picked_plane[:, tokens],
+                    rhs=words.bitcast(FP8X4),
+                    rhs_scale=picked_plane[:, first : first + CHUNK],
                     start=True,
                     stop=True,
                 )
-            return bank
+            return product[:].rearrange("p t j -> p j t")
 
-        gate_slots = staging[:].rearrange("p (s j t) -> p s j t", j=CHUNK, t=PACK)
-        up_woven = keep.tile([P, 2, CHUNK, PACK], F32, name="up_woven")
-        h_rounded = keep.tile([P, (J - 2 * CHUNK) * PACK], BF16, name="h_rounded", align_bytes=64)
-        h_tokens = h_rounded[:].rearrange("p (j t) -> p j t", t=PACK)
-        h_halves = [h_tokens[:, HALF - 2 * CHUNK :, :], h_tokens[:, :HALF, :]]
-
-        def h_woven(first, count):
-            half, inside = divmod(first, HALF)
-            return h_halves[half][:, inside : inside + count, :]
-
+        gate_places = wu_then_gates[:].rearrange("p (s j t) -> p s j t", j=CHUNK, t=PACK)
+        gate_place_of = {}
+        up_woven = keep.tile([P, J // HALF, CHUNK, PACK], F32, name="up_woven")
+        h_rounded = keep.tile([P, (HALF + CHUNK) * PACK], BF16, name="h_rounded", align_bytes=64)
+        h_places = h_rounded[:].rearrange("p (j t) -> p j t", t=PACK)
+        h_halves = [h_places[:, CHUNK:, :], h_places[:, :HALF, :]]
         h_codes = keep.tile([P, J], U32, name="h_codes", align_bytes=64)
         h_plane = keep.tile([P, J], U8, name="h_plane", align_bytes=64)
-        slot_of = {}
 
-        def chunk(c):
-            return slice(c * CHUNK, (c + 1) * CHUNK)
+        def h_chunk(c):
+            half, inside = divmod(c * CHUNK, HALF)
+            return h_halves[half][:, inside : inside + CHUNK, :]
 
         def gate(c, bank):
-            slot_of.setdefault(c, len(slot_of))
-            product = first_product("bank%d" % bank, wg_codes, wg_plane, chunk(c))
-            nc.scalar.activation(
-                gate_slots[:, slot_of[c]], product[:].rearrange("p t j -> p j t"), ACT.Relu
-            )
+            place = gate_place_of.setdefault(c, len(gate_place_of))
+            ga = first_product(bank, wg_codes, wg_plane, c)
+            nc.scalar.activation(gate_places[:, place], ga, ACT.Relu)
 
         def hidden_on_vector(c, bank):
-            up = first_product("bank%d" % bank, wu_codes, wu_plane, chunk(c))
-            nc.vector.tensor_tensor(
-                h_woven(c * CHUNK, CHUNK),
-                gate_slots[:, slot_of[c]],
-                up[:].rearrange("p t j -> p j t"),
-                ALU.mult,
-            )
+            ub = first_product(bank, wu_codes, wu_plane, c)
+            nc.vector.tensor_tensor(h_chunk(c), gate_places[:, gate_place_of[c]], ub, ALU.mult)
 
-        def hidden_on_gpsimd(c, bank, piece):
-            up = first_product("bank%d" % bank, wu_codes, wu_plane, chunk(c))
-            nc.scalar.copy(up_woven[:, c // PACK], up[:].rearrange("p t j -> p j t"))
-            for a in range(0, CHUNK, piece):
-                nc.gpsimd.tensor_tensor(
-                    h_woven(c * CHUNK + a, piece),
-                    gate_slots[:, slot_of[c], a : a + piece, :],
-                    up_woven[:, c // PACK, a : a + piece, :],
-                    ALU.mult,
-                )
+        def hidden_on_gpsimd(c, bank):
+            ub = first_product(bank, wu_codes, wu_plane, c)
+            ub_woven = up_woven[:, c * CHUNK // HALF]
+            nc.scalar.copy(ub_woven, ub)
+            nc.gpsimd.tensor_tensor(h_chunk(c), gate_places[:, gate_place_of[c]], ub_woven, ALU.mult)
 
         def quantise_hidden(half):
             tokens = slice(half * HALF, (half + 1) * HALF)
@@ -202,38 +195,40 @@ def tile_list_gmlpt_relu_resLP_kernel(
                 in_=h_halves[half].rearrange("p j t -> p (j t)"),
             )
 
-        gate(0, 0)
-        gate(1, 1)
-        gate(3, 2)
-        gate(2, 3)
-        hidden_on_vector(0, 4)
-        hidden_on_gpsimd(3, 5, 128)
-        gate(4, 0)
-        hidden_on_vector(1, 6)
-        gate(5, 1)
-        hidden_on_gpsimd(5, 7, 32)
-        hidden_on_vector(2, 2)
-        gate(6, 4)
-        hidden_on_vector(4, 3)
-        gate(7, 6)
+        gate(0, bank=0)
+        gate(1, bank=1)
+        gate(3, bank=2)
+        gate(2, bank=3)
+        hidden_on_vector(0, bank=4)
+        hidden_on_gpsimd(3, bank=5)
+        gate(4, bank=0)
+        hidden_on_vector(1, bank=6)
+        gate(5, bank=1)
+        hidden_on_vector(2, bank=2)
+        gate(6, bank=4)
+        hidden_on_vector(4, bank=3)
+        gate(7, bank=6)
         quantise_hidden(0)
-        hidden_on_vector(6, 5)
-        hidden_on_vector(7, 7)
+        hidden_on_gpsimd(5, bank=7)
+        hidden_on_vector(6, bank=5)
+        hidden_on_vector(7, bank=2)
         quantise_hidden(1)
+        down_banks = (0, 1, 7, 3, 4, 6, 5, 2)
 
-        trail = keep.tile([P, PACK * J], F32, name="trail")
-        first_sums = keep.tile([P, PACK * HALF], F32, name="first_sums")
+        y_then_sums = keep.tile([P, PACK * J], F32, name="y_then_sums")
+        first_sums = keep.tile([P, PACK * OUT_GROUPS[0]], F32, name="first_sums")
         first = 0
-        bank = 0
+        filled = 0
         for width in OUT_GROUPS:
-            tokens = slice(first, first + width)
-            per_bank = HALF // width
-            for t0 in range(0, PACK, per_bank):
-                down = psum.tile([P, per_bank, width], F32, name="down", tag="bank%d" % DOWN_BANKS[bank])
-                bank = bank + 1
-                for u in range(per_bank):
+            slices_per_bank = BANK // width
+            for t0 in range(0, PACK, slices_per_bank):
+                down = psum.tile([P, BANK], F32, name="down", tag="bank%d" % down_banks[filled])
+                pass_width = FIRST_Y_PIECE if filled == 0 else width
+                for lo in range(0, BANK, pass_width):
+                    u, inside = divmod(lo, width)
+                    tokens = slice(first + inside, first + inside + pass_width)
                     nc.tensor.matmul_mx(
-                        out=down[:, u, :],
+                        out=down[:, lo : lo + pass_width],
                         lhsT=wd_codes[:, t0 + u, :].bitcast(FP4X4),
                         lhsT_scale=wd_plane[:, t0 + u, :],
                         rhs=h_codes[:, tokens].bitcast(FP8X4),
@@ -242,40 +237,48 @@ def tile_list_gmlpt_relu_resLP_kernel(
                         stop=True,
                     )
                 at = PACK * first + t0 * width
-                nc.scalar.copy(trail[:, at : at + HALF], down[:].rearrange("p u j -> p (u j)"))
+                copy_width = FIRST_Y_PIECE if filled == 0 else BANK
+                for lo in range(0, BANK, copy_width):
+                    nc.scalar.copy(
+                        y_then_sums[:, at + lo : at + lo + copy_width], down[:, lo : lo + copy_width]
+                    )
+                filled = filled + 1
             first = first + width
 
         out_rows = out_0.rearrange("(p t) j -> p t j", t=PACK)
         out_words = out_1[0].rearrange("p j i -> p (j i)").bitcast(I32)
         out_plane = keep.tile([P, J], U8, name="out_plane", align_bytes=64)
-        woven = keep.tile([P, PACK * J], BF16, name="woven", align_bytes=64)
+        out_rounded = keep.tile([P, PACK * J], BF16, name="out_rounded", align_bytes=64)
         first = 0
         for width in OUT_GROUPS:
-            tokens = slice(first, first + width)
-            base = PACK * first
+            at = PACK * first
             if first == 0:
                 sums = first_sums[:]
             else:
-                sums = trail[:, base - HALF : base - HALF + PACK * width]
+                sums = y_then_sums[:, at - OUT_GROUPS[0] : at - OUT_GROUPS[0] + PACK * width]
             sums = sums.rearrange("p (t j) -> p t j", t=PACK)
-            last = first + width == J
+            last_group = first + width == J
             for t in range(PACK):
-                step = CHUNK if last and t == PACK - 1 else width
-                for a in range(0, width, step):
+                sum_width = width
+                if first == 0 and t == 0:
+                    sum_width = FIRST_Y_PIECE
+                if last_group and t == PACK - 1:
+                    sum_width = CHUNK
+                for lo in range(0, width, sum_width):
                     nc.vector.tensor_tensor(
-                        sums[:, t, a : a + step],
-                        residual[t][:].indirect(list_slice(first + a, step)),
-                        trail[:, base + t * width + a : base + t * width + a + step],
+                        sums[:, t, lo : lo + sum_width],
+                        residual[t][:].indirect(list_slice(first + lo, sum_width)),
+                        y_then_sums[:, at + t * width + lo : at + t * width + lo + sum_width],
                         ALU.add,
                     )
-                nc.sync.dma_start(out=out_rows[:, t, tokens], in_=sums[:, t, :])
-            step = CHUNK if last else width
-            for a in range(0, width, step):
+                nc.sync.dma_start(out=out_rows[:, t, first : first + width], in_=sums[:, t, :])
+            weave_width = CHUNK if last_group else width
+            for lo in range(0, width, weave_width):
                 nc.scalar.copy(
-                    woven[:, PACK * (first + a) : PACK * (first + a + step)].rearrange(
+                    out_rounded[:, PACK * (first + lo) : PACK * (first + lo + weave_width)].rearrange(
                         "p (c i t) -> p c t i", i=4, t=PACK
                     ),
-                    sums[:, :, a : a + step].rearrange("p t (c i) -> p c t i", i=4),
+                    sums[:, :, lo : lo + weave_width].rearrange("p t (c i) -> p c t i", i=4),
                 )
             first = first + width
 
@@ -287,7 +290,7 @@ def tile_list_gmlpt_relu_resLP_kernel(
             nc.vector.quantize_mx(
                 out=out_codes[:, tokens].bitcast(FP8X4),
                 scales=out_plane[:, tokens],
-                in_=woven[:, PACK * first : PACK * (first + width)],
+                in_=out_rounded[:, PACK * first : PACK * (first + width)],
             )
             first = first + width
             if first in WORD_STORE_ENDS:

@@ -30,6 +30,19 @@ OUT_GROUPS = (512, 256, 256)
 FIRST_Y_PIECE = 256
 PLANE_GROUPS = (512, 256, 128, 128)
 WORD_STORE_ENDS = (512, 768, 1024)
+HALF_BYTES = 4 * PACK * R // 2
+PLACE_BYTES = 4 * BANK
+WU_AT = PLACE_BYTES
+LATE_WORDS_AT = 4 * PLACE_BYTES + 64
+WD_PLANE_AT = LATE_WORDS_AT + 4 * (J - EARLY_WORDS)
+WD_CODES_AT = WD_PLANE_AT + N
+PLACES_AT = [32 + u * PLACE_BYTES for u in range(4)] + [
+    WD_CODES_AT + 2 * N + u * PLACE_BYTES for u in range(4)
+]
+Y_PAD = 8
+SUM_ORDERS = ((0, 1, 2, 3), (3, 0, 1, 2), (0, 1, 2, 3))
+Y_PLACES = ((3, 2, 1, 0), (1, 2, 3, 0), (0, 1, 2, 3))
+SUMS_AT = (None, 0, Y_PAD + PACK * OUT_GROUPS[0])
 
 
 def load_scale_rows(queues, plane, rows):
@@ -52,10 +65,11 @@ def tile_list_gmlpt_relu_resLP_kernel(
         offsets = keep.tile([P, J // LIST_ROWS], U16, name="offsets")
         table_words = keep.tile([P, T], I32, name="table_words", align_bytes=64)
         table_plane = keep.tile([P, T], U8, name="table_plane", align_bytes=64)
-        wg_raw = [keep.tile([P, PACK, R // 2], F32, name="wg_raw%d" % a)[:] for a in range(2)]
-        wu_then_gates = keep.tile([P, PACK * J], F32, name="wu_then_gates")
+        wg_raw = [
+            keep.tile([P, PACK, R // 2], F32, name="wg_raw%d" % a, align_bytes=64)[:] for a in range(2)
+        ]
         wu_raw = [
-            wu_then_gates[:, a * 2 * R : (a + 1) * 2 * R].rearrange("p (i r) -> p i r", i=PACK)
+            after_wu.tile([P, PACK, R // 2], F32, name="wu_raw%d" % a, offset=WU_AT + a * HALF_BYTES)[:]
             for a in range(2)
         ]
         wd_raw = keep.tile([P, 2 * N], U8, name="wd_raw", align_bytes=64)
@@ -109,13 +123,13 @@ def tile_list_gmlpt_relu_resLP_kernel(
             return codes, plane
 
         wg_rounded = keep.tile([P, PACK * R], BF16, name="wg_rounded", align_bytes=64)
-        wu_rounded = after_wu.tile([P, PACK * R], BF16, name="wu_rounded", offset=0, align_bytes=64)
+        wu_rounded = keep.tile([P, PACK * R], BF16, name="wu_rounded", align_bytes=64)
         round_columns(nc.scalar.copy, wg_rounded, wg_raw, 0, 0, M_HALF)
         round_columns(nc.scalar.copy, wg_rounded, wg_raw, 1, 0, WG_SCALAR_COLUMNS)
         round_columns(nc.vector.tensor_copy, wg_rounded, wg_raw, 1, WG_SCALAR_COLUMNS, M_HALF)
         wg_codes, wg_plane = quantise_weight(wg_rounded, "wg")
         early_words = keep.tile(
-            [P, EARLY_WORDS], U32, name="early_words", tag="wg_rounded", align_bytes=64
+            [P, EARLY_WORDS], U32, name="early_words", tag="wg_raw1", align_bytes=64
         )
         gather_words(early_words[:, :FIRST_WORDS], 0, FIRST_WORDS)
         gather_words(early_words[:, FIRST_WORDS:], FIRST_WORDS, EARLY_WORDS - FIRST_WORDS)
@@ -123,17 +137,19 @@ def tile_list_gmlpt_relu_resLP_kernel(
         round_columns(nc.vector.tensor_copy, wu_rounded, wu_raw, 1, 0, M_HALF)
         wu_codes, wu_plane = quantise_weight(wu_rounded, "wu")
         late_words = after_wu.tile(
-            [P, J - EARLY_WORDS], U32, name="late_words", offset=0, align_bytes=64
+            [P, J - EARLY_WORDS], U32, name="late_words", offset=LATE_WORDS_AT, align_bytes=64
         )
         gather_words(late_words[:], EARLY_WORDS, J - EARLY_WORDS)
 
-        wd_codes = keep.tile([P, PACK, 2 * P], U8, name="wd_codes", align_bytes=64)
+        wd_codes = after_wu.tile(
+            [P, PACK, 2 * P], U8, name="wd_codes", offset=WD_CODES_AT, align_bytes=64
+        )
         nc.vector.tensor_copy(
             wd_codes[:].bitcast(U16).rearrange("p t m -> p m t"),
             wd_raw[:].bitcast(U16).rearrange("p (m t) -> p m t", t=PACK),
         )
         wd_plane = after_wu.tile(
-            [P, PACK, P], U8, name="wd_plane", offset=4 * (J - EARLY_WORDS), align_bytes=64
+            [P, PACK, P], U8, name="wd_plane", offset=WD_PLANE_AT, align_bytes=64
         )
         nc.vector.tensor_copy(
             wd_plane[:].rearrange("p t m -> p m t"),
@@ -159,12 +175,10 @@ def tile_list_gmlpt_relu_resLP_kernel(
                 )
             return product[:].rearrange("p t j -> p j t")
 
-        gate_places = wu_then_gates[:].rearrange("p (s j t) -> p s j t", j=CHUNK, t=PACK)
-        gate_place_of = {}
-        up_woven = keep.tile([P, J // HALF, CHUNK, PACK], F32, name="up_woven")
-        h_rounded = keep.tile([P, (HALF + CHUNK) * PACK], BF16, name="h_rounded", align_bytes=64)
+        gates = {}
+        h_rounded = keep.tile([P, (J - CHUNK) * PACK], BF16, name="h_rounded", align_bytes=64)
         h_places = h_rounded[:].rearrange("p (j t) -> p j t", t=PACK)
-        h_halves = [h_places[:, CHUNK:, :], h_places[:, :HALF, :]]
+        h_halves = [h_places[:, HALF - CHUNK :, :], h_places[:, :HALF, :]]
         h_codes = keep.tile([P, J], U32, name="h_codes", align_bytes=64)
         h_plane = keep.tile([P, J], U8, name="h_plane", align_bytes=64)
 
@@ -172,20 +186,23 @@ def tile_list_gmlpt_relu_resLP_kernel(
             half, inside = divmod(c * CHUNK, HALF)
             return h_halves[half][:, inside : inside + CHUNK, :]
 
-        def gate(c, bank):
-            place = gate_place_of.setdefault(c, len(gate_place_of))
+        def woven_tile(name, place):
+            return after_wu.tile([P, CHUNK, PACK], F32, name=name, offset=PLACES_AT[place])
+
+        def gate(c, bank, place):
             ga = first_product(bank, wg_codes, wg_plane, c)
-            nc.scalar.activation(gate_places[:, place], ga, ACT.Relu)
+            gates[c] = woven_tile("gate%d" % c, place)
+            nc.scalar.activation(gates[c][:], ga, ACT.Relu)
 
         def hidden_on_vector(c, bank):
             ub = first_product(bank, wu_codes, wu_plane, c)
-            nc.vector.tensor_tensor(h_chunk(c), gate_places[:, gate_place_of[c]], ub, ALU.mult)
+            nc.vector.tensor_tensor(h_chunk(c), gates[c][:], ub, ALU.mult)
 
-        def hidden_on_gpsimd(c, bank):
+        def hidden_on_gpsimd(c, bank, place):
             ub = first_product(bank, wu_codes, wu_plane, c)
-            ub_woven = up_woven[:, c * CHUNK // HALF]
-            nc.scalar.copy(ub_woven, ub)
-            nc.gpsimd.tensor_tensor(h_chunk(c), gate_places[:, gate_place_of[c]], ub_woven, ALU.mult)
+            ub_woven = woven_tile("up%d" % c, place)
+            nc.scalar.copy(ub_woven[:], ub)
+            nc.gpsimd.tensor_tensor(h_chunk(c), gates[c][:], ub_woven[:], ALU.mult)
 
         def quantise_hidden(half):
             tokens = slice(half * HALF, (half + 1) * HALF)
@@ -195,31 +212,31 @@ def tile_list_gmlpt_relu_resLP_kernel(
                 in_=h_halves[half].rearrange("p j t -> p (j t)"),
             )
 
-        gate(0, bank=0)
-        gate(1, bank=1)
-        gate(3, bank=2)
-        gate(2, bank=3)
+        gate(0, bank=0, place=0)
+        gate(1, bank=1, place=1)
+        gate(3, bank=2, place=2)
+        gate(2, bank=3, place=3)
         hidden_on_vector(0, bank=4)
-        hidden_on_gpsimd(3, bank=5)
-        gate(4, bank=0)
+        hidden_on_gpsimd(3, bank=5, place=4)
+        gate(4, bank=0, place=5)
         hidden_on_vector(1, bank=6)
-        gate(5, bank=1)
+        gate(7, bank=1, place=6)
         hidden_on_vector(2, bank=2)
-        gate(6, bank=4)
         hidden_on_vector(4, bank=3)
-        gate(7, bank=6)
         quantise_hidden(0)
-        hidden_on_gpsimd(5, bank=7)
-        hidden_on_vector(6, bank=5)
-        hidden_on_vector(7, bank=2)
+        hidden_on_gpsimd(7, bank=7, place=7)
+        gate(5, bank=4, place=4)
+        gate(6, bank=6, place=2)
+        hidden_on_vector(5, bank=5)
+        hidden_on_vector(6, bank=2)
         quantise_hidden(1)
         down_banks = (0, 1, 7, 3, 4, 6, 5, 2)
 
-        y_then_sums = keep.tile([P, PACK * J], F32, name="y_then_sums")
+        y_then_sums = keep.tile([P, Y_PAD + PACK * J], F32, name="y_then_sums")
         first_sums = keep.tile([P, PACK * OUT_GROUPS[0]], F32, name="first_sums")
         first = 0
         filled = 0
-        for width in OUT_GROUPS:
+        for width, order, places in zip(OUT_GROUPS, SUM_ORDERS, Y_PLACES):
             slices_per_bank = BANK // width
             for t0 in range(0, PACK, slices_per_bank):
                 down = psum.tile([P, BANK], F32, name="down", tag="bank%d" % down_banks[filled])
@@ -229,14 +246,14 @@ def tile_list_gmlpt_relu_resLP_kernel(
                     tokens = slice(first + inside, first + inside + pass_width)
                     nc.tensor.matmul_mx(
                         out=down[:, lo : lo + pass_width],
-                        lhsT=wd_codes[:, t0 + u, :].bitcast(FP4X4),
-                        lhsT_scale=wd_plane[:, t0 + u, :],
+                        lhsT=wd_codes[:, order[t0 + u], :].bitcast(FP4X4),
+                        lhsT_scale=wd_plane[:, order[t0 + u], :],
                         rhs=h_codes[:, tokens].bitcast(FP8X4),
                         rhs_scale=h_plane[:, tokens],
                         start=True,
                         stop=True,
                     )
-                at = PACK * first + t0 * width
+                at = Y_PAD + PACK * first + places[order[t0]] * width
                 copy_width = FIRST_Y_PIECE if filled == 0 else BANK
                 for lo in range(0, BANK, copy_width):
                     nc.scalar.copy(
@@ -250,15 +267,16 @@ def tile_list_gmlpt_relu_resLP_kernel(
         out_plane = keep.tile([P, J], U8, name="out_plane", align_bytes=64)
         out_rounded = keep.tile([P, PACK * J], BF16, name="out_rounded", align_bytes=64)
         first = 0
-        for width in OUT_GROUPS:
-            at = PACK * first
+        for group, width in enumerate(OUT_GROUPS):
+            at = Y_PAD + PACK * first
             if first == 0:
                 sums = first_sums[:]
             else:
-                sums = y_then_sums[:, at - OUT_GROUPS[0] : at - OUT_GROUPS[0] + PACK * width]
+                sums = y_then_sums[:, SUMS_AT[group] : SUMS_AT[group] + PACK * width]
             sums = sums.rearrange("p (t j) -> p t j", t=PACK)
             last_group = first + width == J
-            for t in range(PACK):
+            for t in SUM_ORDERS[group]:
+                y_at = at + Y_PLACES[group][t] * width
                 sum_width = width
                 if first == 0 and t == 0:
                     sum_width = FIRST_Y_PIECE
@@ -268,7 +286,7 @@ def tile_list_gmlpt_relu_resLP_kernel(
                     nc.vector.tensor_tensor(
                         sums[:, t, lo : lo + sum_width],
                         residual[t][:].indirect(list_slice(first + lo, sum_width)),
-                        y_then_sums[:, at + t * width + lo : at + t * width + lo + sum_width],
+                        y_then_sums[:, y_at + lo : y_at + lo + sum_width],
                         ALU.add,
                     )
                 nc.sync.dma_start(out=out_rows[:, t, first : first + width], in_=sums[:, t, :])

@@ -111,15 +111,20 @@ def tile_list_gmlpt_relu_resLP_kernel(
                 picked, table_words[:].bitcast(U32).indirect(list_slice(first, count))
             )
 
-        def round_columns(copy, rounded, raw, a, first, last):
+        def round_columns(copy, rounded, raw, a, first, last, slices=slice(0, PACK)):
             dealt = rounded[:].rearrange("p (t m i) -> p m i t", t=PACK, i=PACK)
             source = raw[a].rearrange("p i (m t) -> p m i t", t=PACK)
-            copy(dealt[:, a * M_HALF + first : a * M_HALF + last], source[:, first:last])
+            copy(dealt[:, a * M_HALF + first : a * M_HALF + last, :, slices], source[:, first:last, :, slices])
 
-        def quantise_weight(rounded, name):
+        def quantise_weight(rounded, name, width):
             codes = keep.tile([P, R], U32, name=name + "_codes", align_bytes=64)
             plane = keep.tile([P, R], U8, name=name + "_plane", align_bytes=64)
-            nc.vector.quantize_mx(out=codes[:].bitcast(FP8X4), scales=plane[:], in_=rounded[:])
+            for lo in range(0, R, width):
+                nc.vector.quantize_mx(
+                    out=codes[:, lo : lo + width].bitcast(FP8X4),
+                    scales=plane[:, lo : lo + width],
+                    in_=rounded[:, PACK * lo : PACK * (lo + width)],
+                )
             return codes, plane
 
         wg_rounded = keep.tile([P, PACK * R], BF16, name="wg_rounded", align_bytes=64)
@@ -127,15 +132,16 @@ def tile_list_gmlpt_relu_resLP_kernel(
         round_columns(nc.scalar.copy, wg_rounded, wg_raw, 0, 0, M_HALF)
         round_columns(nc.scalar.copy, wg_rounded, wg_raw, 1, 0, WG_SCALAR_COLUMNS)
         round_columns(nc.vector.tensor_copy, wg_rounded, wg_raw, 1, WG_SCALAR_COLUMNS, M_HALF)
-        wg_codes, wg_plane = quantise_weight(wg_rounded, "wg")
+        wg_codes, wg_plane = quantise_weight(wg_rounded, "wg", R)
         early_words = keep.tile(
             [P, EARLY_WORDS], U32, name="early_words", tag="wg_raw1", align_bytes=64
         )
         gather_words(early_words[:, :FIRST_WORDS], 0, FIRST_WORDS)
         gather_words(early_words[:, FIRST_WORDS:], FIRST_WORDS, EARLY_WORDS - FIRST_WORDS)
         round_columns(nc.scalar.copy, wu_rounded, wu_raw, 0, 0, M_HALF)
-        round_columns(nc.vector.tensor_copy, wu_rounded, wu_raw, 1, 0, M_HALF)
-        wu_codes, wu_plane = quantise_weight(wu_rounded, "wu")
+        for t in range(0, PACK, 2):
+            round_columns(nc.vector.tensor_copy, wu_rounded, wu_raw, 1, 0, M_HALF, slice(t, t + 2))
+        wu_codes, wu_plane = quantise_weight(wu_rounded, "wu", R // 2)
         late_words = after_wu.tile(
             [P, J - EARLY_WORDS], U32, name="late_words", offset=LATE_WORDS_AT, align_bytes=64
         )
@@ -215,9 +221,9 @@ def tile_list_gmlpt_relu_resLP_kernel(
         gate(0, bank=0, place=0)
         gate(1, bank=1, place=1)
         gate(3, bank=2, place=2)
-        gate(2, bank=3, place=3)
-        hidden_on_vector(0, bank=4)
         hidden_on_gpsimd(3, bank=5, place=4)
+        hidden_on_vector(0, bank=4)
+        gate(2, bank=3, place=3)
         gate(4, bank=0, place=5)
         hidden_on_vector(1, bank=6)
         gate(7, bank=1, place=6)

@@ -34,11 +34,10 @@ HALF_BYTES = 4 * PACK * R // 2
 PLACE_BYTES = 4 * BANK
 WU_AT = PLACE_BYTES
 LATE_WORDS_AT = 4 * PLACE_BYTES + 64
-WD_PLANE_AT = LATE_WORDS_AT + 4 * (J - EARLY_WORDS)
-WD_CODES_AT = WD_PLANE_AT + N
-PLACES_AT = [32 + u * PLACE_BYTES for u in range(4)] + [
-    WD_CODES_AT + 2 * N + u * PLACE_BYTES for u in range(4)
-]
+AFTER_WU = WU_AT + 2 * HALF_BYTES
+PLACES_AT = [32 + u * PLACE_BYTES for u in range(4)] + [AFTER_WU + u * PLACE_BYTES for u in range(4)]
+WU_ROUNDED_AT = AFTER_WU + 4 * PLACE_BYTES
+WD_PLANE_AT = WU_ROUNDED_AT + 2 * PACK * R - N
 Y_PAD = 8
 SUM_ORDERS = ((0, 1, 2, 3), (3, 0, 1, 2), (0, 1, 2, 3))
 Y_PLACES = ((3, 2, 1, 0), (1, 2, 3, 0), (0, 1, 2, 3))
@@ -93,9 +92,9 @@ def tile_list_gmlpt_relu_resLP_kernel(
 
         load_weight(wg_raw, wg)
         nc.sync.dma_start(out=table_words[:, 2 * TABLE_LEAD :], in_=table_rows[:, 2 * TABLE_LEAD :])
-        load_weight(wu_raw, wu)
         nc.sync.dma_start(out=wd_raw[:].bitcast(I32), in_=wd_words[0].bitcast(I32))
         load_scale_rows((nc.sync,), wd_plane_raw, wd_scales[0])
+        load_weight(wu_raw, wu)
         residual_rows = rT.rearrange("(p t) c -> p t c", t=PACK)
         for t in range(PACK):
             nc.sync.dma_start(out=residual[t][:], in_=residual_rows[:, t, :])
@@ -128,7 +127,9 @@ def tile_list_gmlpt_relu_resLP_kernel(
             return codes, plane
 
         wg_rounded = keep.tile([P, PACK * R], BF16, name="wg_rounded", align_bytes=64)
-        wu_rounded = keep.tile([P, PACK * R], BF16, name="wu_rounded", align_bytes=64)
+        wu_rounded = after_wu.tile(
+            [P, PACK * R], BF16, name="wu_rounded", offset=WU_ROUNDED_AT, align_bytes=64
+        )
         round_columns(nc.scalar.copy, wg_rounded, wg_raw, 0, 0, M_HALF)
         round_columns(nc.scalar.copy, wg_rounded, wg_raw, 1, 0, WG_SCALAR_COLUMNS)
         round_columns(nc.vector.tensor_copy, wg_rounded, wg_raw, 1, WG_SCALAR_COLUMNS, M_HALF)
@@ -147,19 +148,15 @@ def tile_list_gmlpt_relu_resLP_kernel(
         )
         gather_words(late_words[:], EARLY_WORDS, J - EARLY_WORDS)
 
-        wd_codes = after_wu.tile(
-            [P, PACK, 2 * P], U8, name="wd_codes", offset=WD_CODES_AT, align_bytes=64
-        )
-        nc.vector.tensor_copy(
-            wd_codes[:].bitcast(U16).rearrange("p t m -> p m t"),
-            wd_raw[:].bitcast(U16).rearrange("p (m t) -> p m t", t=PACK),
+        wd_codes = keep.tile([P, PACK, 2 * P], U8, name="wd_codes", align_bytes=64)
+        nc.scalar.copy(
+            wd_codes[:].bitcast(U16), wd_raw[:].bitcast(U16).rearrange("p (m t) -> p t m", t=PACK)
         )
         wd_plane = after_wu.tile(
             [P, PACK, P], U8, name="wd_plane", offset=WD_PLANE_AT, align_bytes=64
         )
-        nc.vector.tensor_copy(
-            wd_plane[:].rearrange("p t m -> p m t"),
-            wd_plane_raw[:].rearrange("p (m t) -> p m t", t=PACK),
+        nc.gpsimd.tensor_copy(
+            wd_plane[:], wd_plane_raw[:].rearrange("p (m t) -> p t m", t=PACK)
         )
 
         def first_product(bank, codes, plane, c):

@@ -34,7 +34,8 @@ HALF_BYTES = 4 * PACK * R // 2
 PLACE_BYTES = 4 * BANK
 WU_AT = PLACE_BYTES
 LATE_WORDS_AT = 4 * PLACE_BYTES + 64
-AFTER_WU = WU_AT + 2 * HALF_BYTES
+WD_CODES_AT = LATE_WORDS_AT + 4 * (J - EARLY_WORDS)
+AFTER_WU = WD_CODES_AT + 2 * N
 PLACES_AT = [32 + u * PLACE_BYTES for u in range(4)] + [AFTER_WU + u * PLACE_BYTES for u in range(4)]
 WU_ROUNDED_AT = AFTER_WU + 4 * PLACE_BYTES
 WD_PLANE_AT = WU_ROUNDED_AT + 2 * PACK * R - N
@@ -92,9 +93,9 @@ def tile_list_gmlpt_relu_resLP_kernel(
 
         load_weight(wg_raw, wg)
         nc.sync.dma_start(out=table_words[:, 2 * TABLE_LEAD :], in_=table_rows[:, 2 * TABLE_LEAD :])
-        nc.sync.dma_start(out=wd_raw[:].bitcast(I32), in_=wd_words[0].bitcast(I32))
         load_scale_rows((nc.sync,), wd_plane_raw, wd_scales[0])
         load_weight(wu_raw, wu)
+        nc.sync.dma_start(out=wd_raw[:].bitcast(I32), in_=wd_words[0].bitcast(I32))
         residual_rows = rT.rearrange("(p t) c -> p t c", t=PACK)
         for t in range(PACK):
             nc.sync.dma_start(out=residual[t][:], in_=residual_rows[:, t, :])
@@ -132,8 +133,11 @@ def tile_list_gmlpt_relu_resLP_kernel(
         )
         round_columns(nc.scalar.copy, wg_rounded, wg_raw, 0, 0, M_HALF)
         round_columns(nc.scalar.copy, wg_rounded, wg_raw, 1, 0, WG_SCALAR_COLUMNS)
-        round_columns(nc.vector.tensor_copy, wg_rounded, wg_raw, 1, WG_SCALAR_COLUMNS, M_HALF)
-        wg_codes, wg_plane = quantise_weight(wg_rounded, "wg", R)
+        for t in range(0, PACK, 2):
+            round_columns(
+                nc.vector.tensor_copy, wg_rounded, wg_raw, 1, WG_SCALAR_COLUMNS, M_HALF, slice(t, t + 2)
+            )
+        wg_codes, wg_plane = quantise_weight(wg_rounded, "wg", R // 2)
         early_words = keep.tile(
             [P, EARLY_WORDS], U32, name="early_words", tag="wg_raw1", align_bytes=64
         )
@@ -148,8 +152,10 @@ def tile_list_gmlpt_relu_resLP_kernel(
         )
         gather_words(late_words[:], EARLY_WORDS, J - EARLY_WORDS)
 
-        wd_codes = keep.tile([P, PACK, 2 * P], U8, name="wd_codes", align_bytes=64)
-        nc.scalar.copy(
+        wd_codes = after_wu.tile(
+            [P, PACK, 2 * P], U8, name="wd_codes", offset=WD_CODES_AT, align_bytes=64
+        )
+        nc.vector.tensor_copy(
             wd_codes[:].bitcast(U16), wd_raw[:].bitcast(U16).rearrange("p (m t) -> p t m", t=PACK)
         )
         wd_plane = after_wu.tile(

@@ -26,6 +26,8 @@ M_HALF = P // 2
 TABLE_LEAD = 256
 WG_SCALAR_COLUMNS = 40
 FIRST_WORDS, EARLY_WORDS = 256, 768
+WU_SCALAR_COLUMNS = 44
+GPSIMD_LAST_TOKENS = 112
 OUT_GROUPS = (512, 256, 256)
 FIRST_Y_PIECE = 256
 PLANE_GROUPS = (512, 256, 128, 128)
@@ -68,9 +70,10 @@ def tile_list_gmlpt_relu_resLP_kernel(
         wg_raw = [
             keep.tile([P, PACK, R // 2], F32, name="wg_raw%d" % a, align_bytes=64)[:] for a in range(2)
         ]
+        first_place = keep.tile([P, BANK - Y_PAD + PACK * R // 2], F32, name="first_place")
         wu_raw = [
-            after_wu.tile([P, PACK, R // 2], F32, name="wu_raw%d" % a, offset=WU_AT + a * HALF_BYTES)[:]
-            for a in range(2)
+            first_place[:, BANK - Y_PAD :].rearrange("p (i r) -> p i r", i=PACK),
+            after_wu.tile([P, PACK, R // 2], F32, name="wu_raw1", offset=WU_AT + HALF_BYTES)[:],
         ]
         wd_raw = keep.tile([P, 2 * N], U8, name="wd_raw", align_bytes=64)
         wd_plane_raw = keep.tile([P, N], U8, name="wd_plane_raw")
@@ -143,7 +146,11 @@ def tile_list_gmlpt_relu_resLP_kernel(
         )
         gather_words(early_words[:, :FIRST_WORDS], 0, FIRST_WORDS)
         gather_words(early_words[:, FIRST_WORDS:], FIRST_WORDS, EARLY_WORDS - FIRST_WORDS)
-        round_columns(nc.scalar.copy, wu_rounded, wu_raw, 0, 0, M_HALF)
+        round_columns(nc.scalar.copy, wu_rounded, wu_raw, 0, 0, WU_SCALAR_COLUMNS)
+        for t in range(0, PACK, 2):
+            round_columns(
+                nc.vector.tensor_copy, wu_rounded, wu_raw, 0, WU_SCALAR_COLUMNS, M_HALF, slice(t, t + 2)
+            )
         for t in range(0, PACK, 2):
             round_columns(nc.vector.tensor_copy, wu_rounded, wu_raw, 1, 0, M_HALF, slice(t, t + 2))
         wu_codes, wu_plane = quantise_weight(wu_rounded, "wu", R // 2)
@@ -196,22 +203,27 @@ def tile_list_gmlpt_relu_resLP_kernel(
             return h_halves[half][:, inside : inside + CHUNK, :]
 
         def woven_tile(name, place):
-            return after_wu.tile([P, CHUNK, PACK], F32, name=name, offset=PLACES_AT[place])
+            if place == 0:
+                return first_place[:, :BANK].rearrange("p (j t) -> p j t", t=PACK)
+            if place == 1:
+                return first_place[:, BANK : 2 * BANK].rearrange("p (j t) -> p j t", t=PACK)
+            return after_wu.tile([P, CHUNK, PACK], F32, name=name, offset=PLACES_AT[place])[:]
 
         def gate(c, bank, place):
             ga = first_product(bank, wg_codes, wg_plane, c)
             gates[c] = woven_tile("gate%d" % c, place)
-            nc.scalar.activation(gates[c][:], ga, ACT.Relu)
+            nc.scalar.activation(gates[c], ga, ACT.Relu)
 
         def hidden_on_vector(c, bank):
             ub = first_product(bank, wu_codes, wu_plane, c)
-            nc.vector.tensor_tensor(h_chunk(c), gates[c][:], ub, ALU.mult)
+            nc.vector.tensor_tensor(h_chunk(c), gates[c], ub, ALU.mult)
 
-        def hidden_on_gpsimd(c, bank, place):
+        def hidden_on_gpsimd(c, bank, place, tokens=CHUNK):
             ub = first_product(bank, wu_codes, wu_plane, c)
             ub_woven = woven_tile("up%d" % c, place)
-            nc.scalar.copy(ub_woven[:], ub)
-            nc.gpsimd.tensor_tensor(h_chunk(c), gates[c][:], ub_woven[:], ALU.mult)
+            nc.scalar.copy(ub_woven[:, :tokens], ub[:, :tokens])
+            nc.gpsimd.tensor_tensor(h_chunk(c)[:, :tokens], gates[c][:, :tokens], ub_woven[:, :tokens], ALU.mult)
+            return ub
 
         def quantise_hidden(half):
             tokens = slice(half * HALF, (half + 1) * HALF)
@@ -233,10 +245,12 @@ def tile_list_gmlpt_relu_resLP_kernel(
         hidden_on_vector(2, bank=2)
         hidden_on_vector(4, bank=3)
         quantise_hidden(0)
-        hidden_on_gpsimd(7, bank=7, place=7)
+        last_up = hidden_on_gpsimd(7, bank=7, place=7, tokens=GPSIMD_LAST_TOKENS)
         gate(5, bank=4, place=4)
         gate(6, bank=6, place=2)
         hidden_on_vector(5, bank=5)
+        rest = slice(GPSIMD_LAST_TOKENS, CHUNK)
+        nc.vector.tensor_tensor(h_chunk(7)[:, rest], gates[7][:, rest], last_up[:, rest], ALU.mult)
         hidden_on_vector(6, bank=2)
         quantise_hidden(1)
         down_banks = (0, 1, 7, 3, 4, 6, 5, 2)

@@ -41,10 +41,10 @@ AFTER_WU = WD_CODES_AT + 2 * N
 PLACES_AT = [32 + u * PLACE_BYTES for u in range(4)] + [AFTER_WU + u * PLACE_BYTES for u in range(4)]
 WU_ROUNDED_AT = AFTER_WU + 4 * PLACE_BYTES
 WD_PLANE_AT = WU_ROUNDED_AT + 2 * PACK * R - N
-Y_PAD = 8
-SUM_ORDERS = ((0, 1, 2, 3), (3, 0, 1, 2), (0, 1, 2, 3))
-Y_PLACES = ((3, 2, 1, 0), (1, 2, 3, 0), (0, 1, 2, 3))
-SUMS_AT = (None, 0, Y_PAD + PACK * OUT_GROUPS[0])
+OVERLAP = 8
+Y_PAD = OUT_GROUPS[1]
+Y_PLACES = ((3, 2, 1, 0), (0, 1, 2, 3), (0, 1, 2, 3))
+SUMS_AT = (None, 0, Y_PAD + PACK * OUT_GROUPS[0] + OVERLAP)
 
 
 def load_scale_rows(queues, plane, rows):
@@ -70,9 +70,9 @@ def tile_list_gmlpt_relu_resLP_kernel(
         wg_raw = [
             keep.tile([P, PACK, R // 2], F32, name="wg_raw%d" % a, align_bytes=64)[:] for a in range(2)
         ]
-        first_place = keep.tile([P, BANK - Y_PAD + PACK * R // 2], F32, name="first_place")
+        first_place = keep.tile([P, BANK - OVERLAP + PACK * R // 2], F32, name="first_place")
         wu_raw = [
-            first_place[:, BANK - Y_PAD :].rearrange("p (i r) -> p i r", i=PACK),
+            first_place[:, BANK - OVERLAP :].rearrange("p (i r) -> p i r", i=PACK),
             after_wu.tile([P, PACK, R // 2], F32, name="wu_raw1", offset=WU_AT + HALF_BYTES)[:],
         ]
         wd_raw = keep.tile([P, 2 * N], U8, name="wd_raw", align_bytes=64)
@@ -253,75 +253,89 @@ def tile_list_gmlpt_relu_resLP_kernel(
         nc.vector.tensor_tensor(h_chunk(7)[:, rest], gates[7][:, rest], last_up[:, rest], ALU.mult)
         hidden_on_vector(6, bank=2)
         quantise_hidden(1)
-        down_banks = (0, 1, 7, 3, 4, 6, 5, 2)
 
         y_then_sums = keep.tile([P, Y_PAD + PACK * J], F32, name="y_then_sums")
         first_sums = keep.tile([P, PACK * OUT_GROUPS[0]], F32, name="first_sums")
-        first = 0
-        filled = 0
-        for width, order, places in zip(OUT_GROUPS, SUM_ORDERS, Y_PLACES):
-            slices_per_bank = BANK // width
-            for t0 in range(0, PACK, slices_per_bank):
-                down = psum.tile([P, BANK], F32, name="down", tag="bank%d" % down_banks[filled])
-                pass_width = FIRST_Y_PIECE if filled == 0 else width
-                for lo in range(0, BANK, pass_width):
-                    u, inside = divmod(lo, width)
-                    tokens = slice(first + inside, first + inside + pass_width)
-                    nc.tensor.matmul_mx(
-                        out=down[:, lo : lo + pass_width],
-                        lhsT=wd_codes[:, order[t0 + u], :].bitcast(FP4X4),
-                        lhsT_scale=wd_plane[:, order[t0 + u], :],
-                        rhs=h_codes[:, tokens].bitcast(FP8X4),
-                        rhs_scale=h_plane[:, tokens],
-                        start=True,
-                        stop=True,
-                    )
-                at = Y_PAD + PACK * first + places[order[t0]] * width
-                copy_width = FIRST_Y_PIECE if filled == 0 else BANK
-                for lo in range(0, BANK, copy_width):
-                    nc.scalar.copy(
-                        y_then_sums[:, at + lo : at + lo + copy_width], down[:, lo : lo + copy_width]
-                    )
-                filled = filled + 1
-            first = first + width
+        starts = [sum(OUT_GROUPS[:g]) for g in range(len(OUT_GROUPS))]
+
+        def y_slice(group, t):
+            at = Y_PAD + PACK * starts[group] + Y_PLACES[group][t] * OUT_GROUPS[group]
+            return at, y_then_sums[:, at : at + OUT_GROUPS[group]]
+
+        def down(group, t0, bank, piece=BANK):
+            width = OUT_GROUPS[group]
+            product = psum.tile([P, BANK], F32, name="down", tag="bank%d" % bank)
+            pass_width = min(width, piece)
+            for lo in range(0, BANK, pass_width):
+                u, inside = divmod(lo, width)
+                tokens = slice(starts[group] + inside, starts[group] + inside + pass_width)
+                nc.tensor.matmul_mx(
+                    out=product[:, lo : lo + pass_width],
+                    lhsT=wd_codes[:, t0 + u, :].bitcast(FP4X4),
+                    lhsT_scale=wd_plane[:, t0 + u, :],
+                    rhs=h_codes[:, tokens].bitcast(FP8X4),
+                    rhs_scale=h_plane[:, tokens],
+                    start=True,
+                    stop=True,
+                )
+            at = y_slice(group, t0)[0]
+            for lo in range(0, BANK, piece):
+                nc.scalar.copy(y_then_sums[:, at + lo : at + lo + piece], product[:, lo : lo + piece])
+
+        down(0, 0, 0, piece=FIRST_Y_PIECE)
+        down(0, 1, 1)
+        down(0, 2, 7)
+        down(1, 0, 3)
+        down(0, 3, 3)
+        down(1, 2, 4)
+        down(2, 0, 6)
+        down(2, 2, 5)
 
         out_rows = out_0.rearrange("(p t) j -> p t j", t=PACK)
         out_words = out_1[0].rearrange("p j i -> p (j i)").bitcast(I32)
         out_plane = keep.tile([P, J], U8, name="out_plane", align_bytes=64)
         out_rounded = keep.tile([P, PACK * J], BF16, name="out_rounded", align_bytes=64)
-        first = 0
-        for group, width in enumerate(OUT_GROUPS):
-            at = Y_PAD + PACK * first
-            if first == 0:
-                sums = first_sums[:]
-            else:
-                sums = y_then_sums[:, SUMS_AT[group] : SUMS_AT[group] + PACK * width]
-            sums = sums.rearrange("p (t j) -> p t j", t=PACK)
-            last_group = first + width == J
-            for t in SUM_ORDERS[group]:
-                y_at = at + Y_PLACES[group][t] * width
-                sum_width = width
-                if first == 0 and t == 0:
-                    sum_width = FIRST_Y_PIECE
-                if last_group and t == PACK - 1:
-                    sum_width = CHUNK
-                for lo in range(0, width, sum_width):
-                    nc.vector.tensor_tensor(
-                        sums[:, t, lo : lo + sum_width],
-                        residual[t][:].indirect(list_slice(first + lo, sum_width)),
-                        y_then_sums[:, y_at + lo : y_at + lo + sum_width],
-                        ALU.add,
-                    )
-                nc.sync.dma_start(out=out_rows[:, t, first : first + width], in_=sums[:, t, :])
-            weave_width = CHUNK if last_group else width
-            for lo in range(0, width, weave_width):
+        sums = [first_sums[:].rearrange("p (t j) -> p t j", t=PACK)] + [
+            y_then_sums[:, SUMS_AT[g] : SUMS_AT[g] + PACK * OUT_GROUPS[g]].rearrange("p (t j) -> p t j", t=PACK)
+            for g in (1, 2)
+        ]
+
+        def add_residual(group, t, piece=None):
+            width = OUT_GROUPS[group]
+            piece = piece or width
+            for lo in range(0, width, piece):
+                nc.vector.tensor_tensor(
+                    sums[group][:, t, lo : lo + piece],
+                    residual[t][:].indirect(list_slice(starts[group] + lo, piece)),
+                    y_slice(group, t)[1][:, lo : lo + piece],
+                    ALU.add,
+                )
+            nc.sync.dma_start(
+                out=out_rows[:, t, starts[group] : starts[group] + width], in_=sums[group][:, t, :]
+            )
+
+        def weave(group, piece):
+            for lo in range(0, OUT_GROUPS[group], piece):
+                first = starts[group] + lo
                 nc.scalar.copy(
-                    out_rounded[:, PACK * (first + lo) : PACK * (first + lo + weave_width)].rearrange(
+                    out_rounded[:, PACK * first : PACK * (first + piece)].rearrange(
                         "p (c i t) -> p c t i", i=4, t=PACK
                     ),
-                    sums[:, :, lo : lo + weave_width].rearrange("p t (c i) -> p c t i", i=4),
+                    sums[group][:, :, lo : lo + piece].rearrange("p t (c i) -> p c t i", i=4),
                 )
-            first = first + width
+
+        add_residual(0, 0, piece=FIRST_Y_PIECE)
+        add_residual(0, 1)
+        add_residual(0, 2)
+        add_residual(1, 0)
+        add_residual(0, 3)
+        weave(0, OUT_GROUPS[0])
+        for t in (3, 1, 2):
+            add_residual(1, t)
+        weave(1, OUT_GROUPS[1])
+        for t in range(PACK):
+            add_residual(2, t, piece=CHUNK if t == PACK - 1 else None)
+        weave(2, CHUNK)
 
         out_codes = keep.tile([P, J], I32, name="out_codes", align_bytes=64)
         first = 0

@@ -25,7 +25,8 @@ HALF = J // 2
 M_HALF = P // 2
 TABLE_LEAD = 256
 WG_SCALAR_COLUMNS = 40
-FIRST_WORDS, EARLY_WORDS = 256, 768
+WORD_GATHERS = (128, 384, 256)
+EARLY_WORDS = sum(WORD_GATHERS)
 WU_SCALAR_COLUMNS = 44
 GPSIMD_LAST_TOKENS = 112
 OUT_GROUPS = (512, 256, 256)
@@ -87,7 +88,7 @@ def tile_list_gmlpt_relu_resLP_kernel(
         for a in range(2):
             lead = slice(a * TABLE_LEAD, (a + 1) * TABLE_LEAD)
             nc.sync.dma_start(out=table_words[:, lead], in_=table_rows[:, lead])
-        load_scale_rows((nc.sync, nc.scalar), table_plane, tab_scales[0])
+        load_scale_rows((nc.sync,), table_plane, tab_scales[0])
 
         def load_weight(raw, w):
             rows = w.rearrange("(p i) r -> p i r", i=PACK)
@@ -144,8 +145,10 @@ def tile_list_gmlpt_relu_resLP_kernel(
         early_words = keep.tile(
             [P, EARLY_WORDS], U32, name="early_words", tag="wg_raw1", align_bytes=64
         )
-        gather_words(early_words[:, :FIRST_WORDS], 0, FIRST_WORDS)
-        gather_words(early_words[:, FIRST_WORDS:], FIRST_WORDS, EARLY_WORDS - FIRST_WORDS)
+        first = 0
+        for width in WORD_GATHERS:
+            gather_words(early_words[:, first : first + width], first, width)
+            first = first + width
         round_columns(nc.scalar.copy, wu_rounded, wu_raw, 0, 0, WU_SCALAR_COLUMNS)
         for t in range(0, PACK, 2):
             round_columns(

@@ -80,25 +80,24 @@ def tile_list_gmlpt_relu_resLP_kernel(
         wd_plane_raw = keep.tile([P, N], U8, name="wd_plane_raw")
         residual = [keep.tile([P, T], F32, name="residual%d" % t) for t in range(PACK)]
 
-        nc.vector.memset(table_plane[:].bitcast(I32), 0)
+        nc.gpsimd.memset(table_plane[:].bitcast(I32), 0)
         nc.gpsimd.memset(wd_plane_raw[:].bitcast(I32), 0)
 
         nc.sync.dma_start(offsets[:], offs)
-        table_rows = tab_words[0].rearrange("p t i -> p (t i)").bitcast(I32)
-        for a in range(2):
-            lead = slice(a * TABLE_LEAD, (a + 1) * TABLE_LEAD)
-            nc.sync.dma_start(out=table_words[:, lead], in_=table_rows[:, lead])
-        load_scale_rows((nc.sync,), table_plane, tab_scales[0])
 
-        def load_weight(raw, w):
+        def load_half(raw, w, a):
             rows = w.rearrange("(p i) r -> p i r", i=PACK)
-            for a in range(2):
-                nc.sync.dma_start(out=raw[a], in_=rows[:, :, a * (R // 2) : (a + 1) * (R // 2)])
+            nc.sync.dma_start(out=raw[a], in_=rows[:, :, a * (R // 2) : (a + 1) * (R // 2)])
 
-        load_weight(wg_raw, wg)
-        nc.sync.dma_start(out=table_words[:, 2 * TABLE_LEAD :], in_=table_rows[:, 2 * TABLE_LEAD :])
+        load_half(wg_raw, wg, 0)
+        load_scale_rows((nc.sync,), table_plane, tab_scales[0])
+        load_half(wg_raw, wg, 1)
+        nc.sync.dma_start(
+            out=table_words[:], in_=tab_words[0].rearrange("p t i -> p (t i)").bitcast(I32)
+        )
         load_scale_rows((nc.sync,), wd_plane_raw, wd_scales[0])
-        load_weight(wu_raw, wu)
+        for a in range(2):
+            load_half(wu_raw, wu, a)
         nc.sync.dma_start(out=wd_raw[:].bitcast(I32), in_=wd_words[0].bitcast(I32))
         residual_rows = rT.rearrange("(p t) c -> p t c", t=PACK)
         for t in range(PACK):
@@ -136,11 +135,7 @@ def tile_list_gmlpt_relu_resLP_kernel(
             [P, PACK * R], BF16, name="wu_rounded", offset=WU_ROUNDED_AT, align_bytes=64
         )
         round_columns(nc.scalar.copy, wg_rounded, wg_raw, 0, 0, M_HALF)
-        round_columns(nc.scalar.copy, wg_rounded, wg_raw, 1, 0, WG_SCALAR_COLUMNS)
-        for t in range(0, PACK, 2):
-            round_columns(
-                nc.vector.tensor_copy, wg_rounded, wg_raw, 1, WG_SCALAR_COLUMNS, M_HALF, slice(t, t + 2)
-            )
+        round_columns(nc.scalar.copy, wg_rounded, wg_raw, 1, 0, M_HALF)
         wg_codes, wg_plane = quantise_weight(wg_rounded, "wg", R // 2)
         early_words = keep.tile(
             [P, EARLY_WORDS], U32, name="early_words", tag="wg_raw1", align_bytes=64
@@ -331,8 +326,8 @@ def tile_list_gmlpt_relu_resLP_kernel(
         add_residual(0, 1)
         add_residual(0, 2)
         add_residual(1, 0)
-        add_residual(0, 3)
-        weave(0, OUT_GROUPS[0])
+        add_residual(0, 3, piece=FIRST_Y_PIECE)
+        weave(0, FIRST_Y_PIECE)
         for t in (3, 1, 2):
             add_residual(1, t)
         weave(1, OUT_GROUPS[1])

@@ -43,9 +43,9 @@ PLACES_AT = [32 + u * PLACE_BYTES for u in range(4)] + [AFTER_WU + u * PLACE_BYT
 WU_ROUNDED_AT = AFTER_WU + 4 * PLACE_BYTES
 WD_PLANE_AT = WU_ROUNDED_AT + 2 * PACK * R - N
 OVERLAP = 8
-Y_PAD = OUT_GROUPS[1]
-Y_PLACES = ((3, 2, 1, 0), (0, 1, 2, 3), (0, 1, 2, 3))
-SUMS_AT = (None, 0, Y_PAD + PACK * OUT_GROUPS[0] + OVERLAP)
+Y_PAD = 2 * OUT_GROUPS[1]
+Y_PLACES = ((3, 2, 1, 0), (2, 3, 0, 1), (0, 1, 2, 3))
+SUMS_AT = (None, 0, Y_PAD + PACK * OUT_GROUPS[0] - OVERLAP)
 
 
 def load_scale_rows(queues, plane, rows):
@@ -326,9 +326,10 @@ def tile_list_gmlpt_relu_resLP_kernel(
         add_residual(0, 1)
         add_residual(0, 2)
         add_residual(1, 0)
+        add_residual(1, 1)
         add_residual(0, 3, piece=FIRST_Y_PIECE)
         weave(0, FIRST_Y_PIECE)
-        for t in (3, 1, 2):
+        for t in (2, 3):
             add_residual(1, t)
         weave(1, OUT_GROUPS[1])
         for t in range(PACK):

@@ -49,10 +49,10 @@ SUMS_AT = (None, 0, Y_PAD + PACK * OUT_GROUPS[0] - OVERLAP)
 
 
 def load_scale_rows(queues, plane, rows):
-    for q in range(4):
-        queues[q % len(queues)].dma_start(
-            out=plane[32 * q : 32 * q + 4, :].bitcast(I32),
-            in_=rows[4 * q : 4 * q + 4, :].bitcast(I32),
+    for r in range(4):
+        queues[r % len(queues)].dma_start(
+            out=plane[r:P:32, :].bitcast(I32),
+            in_=rows[r:16:4, :].bitcast(I32),
         )
 
 
@@ -350,9 +350,9 @@ def tile_list_gmlpt_relu_resLP_kernel(
             if first in WORD_STORE_ENDS:
                 nc.sync.dma_start(out=out_words[:, stored:first], in_=out_codes[:, stored:first])
                 stored = first
-        for q in range(4):
-            queue = nc.scalar if q % 2 == 0 else nc.sync
+        for r in range(4):
+            queue = nc.scalar if r % 2 == 0 else nc.sync
             queue.dma_start(
-                out=out_2[0][4 * q : 4 * q + 4, :].bitcast(I32),
-                in_=out_plane[32 * q : 32 * q + 4, :].bitcast(I32),
+                out=out_2[0][r:16:4, :].bitcast(I32),
+                in_=out_plane[r:P:32, :].bitcast(I32),
             )

@@ -83,13 +83,13 @@ def tile_list_gmlpt_relu_resLP_kernel(
         nc.gpsimd.memset(table_plane[:].bitcast(I32), 0)
         nc.gpsimd.memset(wd_plane_raw[:].bitcast(I32), 0)
 
-        nc.sync.dma_start(offsets[:], offs)
 
         def load_half(raw, w, a):
             rows = w.rearrange("(p i) r -> p i r", i=PACK)
             nc.sync.dma_start(out=raw[a], in_=rows[:, :, a * (R // 2) : (a + 1) * (R // 2)])
 
         load_half(wg_raw, wg, 0)
+        nc.sync.dma_start(offsets[:], offs)
         load_scale_rows((nc.sync,), table_plane, tab_scales[0])
         load_half(wg_raw, wg, 1)
         nc.sync.dma_start(

@@ -25,7 +25,7 @@ HALF = J // 2
 M_HALF = P // 2
 TABLE_LEAD = 256
 WG_SCALAR_COLUMNS = 40
-WORD_GATHERS = (128, 384, 256)
+WORD_GATHERS = (128, 128, 256, 256)
 EARLY_WORDS = sum(WORD_GATHERS)
 WU_SCALAR_COLUMNS = 44
 GPSIMD_LAST_TOKENS = 112

@@ -152,17 +152,17 @@ def tile_list_gmlpt_relu_resLP_kernel(
         for t in range(0, PACK, 2):
             round_columns(nc.vector.tensor_copy, wu_rounded, wu_raw, 1, 0, M_HALF, slice(t, t + 2))
         wu_codes, wu_plane = quantise_weight(wu_rounded, "wu", R // 2)
-        late_words = after_wu.tile(
-            [P, J - EARLY_WORDS], U32, name="late_words", offset=LATE_WORDS_AT, align_bytes=64
-        )
-        gather_words(late_words[:], EARLY_WORDS, J - EARLY_WORDS)
-
         wd_codes = after_wu.tile(
             [P, PACK, 2 * P], U8, name="wd_codes", offset=WD_CODES_AT, align_bytes=64
         )
         nc.vector.tensor_copy(
             wd_codes[:].bitcast(U16), wd_raw[:].bitcast(U16).rearrange("p (m t) -> p t m", t=PACK)
         )
+        late_words = after_wu.tile(
+            [P, J - EARLY_WORDS], U32, name="late_words", offset=LATE_WORDS_AT, align_bytes=64
+        )
+        gather_words(late_words[:], EARLY_WORDS, J - EARLY_WORDS)
+
         wd_plane = after_wu.tile(
             [P, PACK, P], U8, name="wd_plane", offset=WD_PLANE_AT, align_bytes=64
         )
@@ -192,7 +192,7 @@ def tile_list_gmlpt_relu_resLP_kernel(
         gates = {}
         h_rounded = keep.tile([P, (J - CHUNK) * PACK], BF16, name="h_rounded", align_bytes=64)
         h_places = h_rounded[:].rearrange("p (j t) -> p j t", t=PACK)
-        h_halves = [h_places[:, HALF - CHUNK :, :], h_places[:, :HALF, :]]
+        h_halves = [h_places[:, :HALF, :], h_places[:, HALF - CHUNK :, :]]
         h_codes = keep.tile([P, J], U32, name="h_codes", align_bytes=64)
         h_plane = keep.tile([P, J], U8, name="h_plane", align_bytes=64)
 
@@ -237,19 +237,19 @@ def tile_list_gmlpt_relu_resLP_kernel(
         hidden_on_gpsimd(3, bank=5, place=4)
         hidden_on_vector(0, bank=4)
         gate(2, bank=3, place=3)
-        gate(4, bank=0, place=5)
+        gate(5, bank=0, place=5)
         hidden_on_vector(1, bank=6)
-        gate(7, bank=1, place=6)
+        gate(4, bank=1, place=6)
         hidden_on_vector(2, bank=2)
-        hidden_on_vector(4, bank=3)
+        hidden_on_vector(5, bank=3)
         quantise_hidden(0)
-        last_up = hidden_on_gpsimd(7, bank=7, place=7, tokens=GPSIMD_LAST_TOKENS)
-        gate(5, bank=4, place=4)
-        gate(6, bank=6, place=2)
-        hidden_on_vector(5, bank=5)
+        last_up = hidden_on_gpsimd(4, bank=7, place=7, tokens=GPSIMD_LAST_TOKENS)
+        gate(6, bank=4, place=4)
+        gate(7, bank=6, place=2)
+        hidden_on_vector(6, bank=5)
         rest = slice(GPSIMD_LAST_TOKENS, CHUNK)
-        nc.vector.tensor_tensor(h_chunk(7)[:, rest], gates[7][:, rest], last_up[:, rest], ALU.mult)
-        hidden_on_vector(6, bank=2)
+        nc.vector.tensor_tensor(h_chunk(4)[:, rest], gates[4][:, rest], last_up[:, rest], ALU.mult)
+        hidden_on_vector(7, bank=2)
         quantise_hidden(1)
 
         y_then_sums = keep.tile([P, Y_PAD + PACK * J], F32, name="y_then_sums")

@@ -243,12 +243,10 @@ def tile_list_gmlpt_relu_resLP_kernel(
         hidden_on_vector(2, bank=2)
         hidden_on_vector(5, bank=3)
         quantise_hidden(0)
-        last_up = hidden_on_gpsimd(4, bank=7, place=7, tokens=GPSIMD_LAST_TOKENS)
+        hidden_on_gpsimd(4, bank=7, place=7)
         gate(6, bank=4, place=4)
         gate(7, bank=6, place=2)
         hidden_on_vector(6, bank=5)
-        rest = slice(GPSIMD_LAST_TOKENS, CHUNK)
-        nc.vector.tensor_tensor(h_chunk(4)[:, rest], gates[4][:, rest], last_up[:, rest], ALU.mult)
         hidden_on_vector(7, bank=2)
         quantise_hidden(1)
 

@@ -25,7 +25,7 @@ HALF = J // 2
 M_HALF = P // 2
 TABLE_LEAD = 256
 WG_SCALAR_COLUMNS = 40
-WORD_GATHERS = (128, 128, 256, 256)
+WORD_GATHERS = (128, 128, 256, 128)
 EARLY_WORDS = sum(WORD_GATHERS)
 WU_SCALAR_COLUMNS = 44
 GPSIMD_LAST_TOKENS = 112
@@ -144,6 +144,10 @@ def tile_list_gmlpt_relu_resLP_kernel(
         for width in WORD_GATHERS:
             gather_words(early_words[:, first : first + width], first, width)
             first = first + width
+        wd_plane = keep.tile([P, PACK, P], U8, name="wd_plane", tag="wg_rounded", align_bytes=64)
+        nc.gpsimd.tensor_copy(
+            wd_plane[:], wd_plane_raw[:].rearrange("p (m t) -> p t m", t=PACK)
+        )
         round_columns(nc.scalar.copy, wu_rounded, wu_raw, 0, 0, WU_SCALAR_COLUMNS)
         for t in range(0, PACK, 2):
             round_columns(
@@ -153,22 +157,17 @@ def tile_list_gmlpt_relu_resLP_kernel(
             round_columns(nc.vector.tensor_copy, wu_rounded, wu_raw, 1, 0, M_HALF, slice(t, t + 2))
         wu_codes, wu_plane = quantise_weight(wu_rounded, "wu", R // 2)
         wd_codes = after_wu.tile(
-            [P, PACK, 2 * P], U8, name="wd_codes", offset=WD_CODES_AT, align_bytes=64
+            [P, PACK, 2 * P], U8, name="wd_codes", offset=WU_ROUNDED_AT, align_bytes=64
         )
-        nc.vector.tensor_copy(
-            wd_codes[:].bitcast(U16), wd_raw[:].bitcast(U16).rearrange("p (m t) -> p t m", t=PACK)
+        nc.gpsimd.tensor_copy(
+            wd_codes[:].rearrange("p t (m b) -> p t m b", b=2),
+            wd_raw[:].rearrange("p (m t b) -> p t m b", t=PACK, b=2),
         )
         late_words = after_wu.tile(
             [P, J - EARLY_WORDS], U32, name="late_words", offset=LATE_WORDS_AT, align_bytes=64
         )
         gather_words(late_words[:], EARLY_WORDS, J - EARLY_WORDS)
 
-        wd_plane = after_wu.tile(
-            [P, PACK, P], U8, name="wd_plane", offset=WD_PLANE_AT, align_bytes=64
-        )
-        nc.gpsimd.tensor_copy(
-            wd_plane[:], wd_plane_raw[:].rearrange("p (m t) -> p t m", t=PACK)
-        )
 
         def first_product(bank, codes, plane, c):
             first = c * CHUNK
@@ -192,7 +191,7 @@ def tile_list_gmlpt_relu_resLP_kernel(
         gates = {}
         h_rounded = keep.tile([P, (J - CHUNK) * PACK], BF16, name="h_rounded", align_bytes=64)
         h_places = h_rounded[:].rearrange("p (j t) -> p j t", t=PACK)
-        h_halves = [h_places[:, :HALF, :], h_places[:, HALF - CHUNK :, :]]
+        h_halves = [h_places[:, HALF - CHUNK :, :], h_places[:, :HALF, :]]
         h_codes = keep.tile([P, J], U32, name="h_codes", align_bytes=64)
         h_plane = keep.tile([P, J], U8, name="h_plane", align_bytes=64)
 
@@ -237,17 +236,17 @@ def tile_list_gmlpt_relu_resLP_kernel(
         hidden_on_gpsimd(3, bank=5, place=4)
         hidden_on_vector(0, bank=4)
         gate(2, bank=3, place=3)
-        gate(5, bank=0, place=5)
+        gate(4, bank=0, place=5)
         hidden_on_vector(1, bank=6)
-        gate(4, bank=1, place=6)
         hidden_on_vector(2, bank=2)
-        hidden_on_vector(5, bank=3)
+        gate(7, bank=1, place=6)
+        hidden_on_vector(4, bank=3)
         quantise_hidden(0)
-        hidden_on_gpsimd(4, bank=7, place=7)
-        gate(6, bank=4, place=4)
-        gate(7, bank=6, place=2)
-        hidden_on_vector(6, bank=5)
-        hidden_on_vector(7, bank=2)
+        hidden_on_gpsimd(7, bank=7, place=7)
+        gate(5, bank=4, place=4)
+        gate(6, bank=6, place=2)
+        hidden_on_vector(5, bank=5)
+        hidden_on_vector(6, bank=2)
         quantise_hidden(1)
 
         y_then_sums = keep.tile([P, Y_PAD + PACK * J], F32, name="y_then_sums")

@@ -27,7 +27,7 @@ TABLE_LEAD = 256
 WG_SCALAR_COLUMNS = 40
 WORD_GATHERS = (128, 128, 256, 128)
 EARLY_WORDS = sum(WORD_GATHERS)
-WU_SCALAR_COLUMNS = 44
+WU_SCALAR_COLUMNS = 32
 GPSIMD_LAST_TOKENS = 112
 OUT_GROUPS = (512, 256, 256)
 FIRST_Y_PIECE = 256
@@ -236,9 +236,9 @@ def tile_list_gmlpt_relu_resLP_kernel(
         hidden_on_gpsimd(3, bank=5, place=4)
         hidden_on_vector(0, bank=4)
         gate(2, bank=3, place=3)
-        gate(4, bank=0, place=5)
+        gate(4, bank=2, place=5)
         hidden_on_vector(1, bank=6)
-        hidden_on_vector(2, bank=2)
+        hidden_on_vector(2, bank=0)
         gate(7, bank=1, place=6)
         hidden_on_vector(4, bank=3)
         quantise_hidden(0)

@@ -33,6 +33,7 @@ OUT_GROUPS = (512, 256, 256)
 FIRST_Y_PIECE = 256
 PLANE_GROUPS = (512, 256, 128, 128)
 WORD_STORE_ENDS = (512, 768, 1024)
+DMA_ALIGN = 256
 HALF_BYTES = 4 * PACK * R // 2
 PLACE_BYTES = 4 * BANK
 WU_AT = PLACE_BYTES
@@ -66,19 +67,20 @@ def tile_list_gmlpt_relu_resLP_kernel(
         psum = ctx.enter_context(tc.psum_pool(name="psum", bufs=1))
 
         offsets = keep.tile([P, J // LIST_ROWS], U16, name="offsets")
-        table_words = keep.tile([P, T], I32, name="table_words", align_bytes=64)
-        table_plane = keep.tile([P, T], U8, name="table_plane", align_bytes=64)
+        table_words = keep.tile([P, T], I32, name="table_words", align_bytes=DMA_ALIGN)
+        table_plane = keep.tile([P, T], U8, name="table_plane", align_bytes=DMA_ALIGN)
         wg_raw = [
-            keep.tile([P, PACK, R // 2], F32, name="wg_raw%d" % a, align_bytes=64)[:] for a in range(2)
+            keep.tile([P, PACK, R // 2], F32, name="wg_raw%d" % a, align_bytes=DMA_ALIGN)[:] for a in range(2)
         ]
-        first_place = keep.tile([P, BANK - OVERLAP + PACK * R // 2], F32, name="first_place")
+        first_space = keep.tile([P, BANK + PACK * R // 2], F32, name="first_space", align_bytes=DMA_ALIGN)
+        first_place = first_space[:, OVERLAP:]
         wu_raw = [
             first_place[:, BANK - OVERLAP :].rearrange("p (i r) -> p i r", i=PACK),
-            after_wu.tile([P, PACK, R // 2], F32, name="wu_raw1", offset=WU_AT + HALF_BYTES)[:],
+            after_wu.tile([P, PACK, R // 2], F32, name="wu_raw1", offset=WU_AT + HALF_BYTES, align_bytes=DMA_ALIGN)[:],
         ]
-        wd_raw = keep.tile([P, 2 * N], U8, name="wd_raw", align_bytes=64)
-        wd_plane_raw = keep.tile([P, N], U8, name="wd_plane_raw")
-        residual = [keep.tile([P, T], F32, name="residual%d" % t) for t in range(PACK)]
+        wd_raw = keep.tile([P, 2 * N], U8, name="wd_raw", align_bytes=DMA_ALIGN)
+        wd_plane_raw = keep.tile([P, N], U8, name="wd_plane_raw", align_bytes=DMA_ALIGN)
+        residual = [keep.tile([P, T], F32, name="residual%d" % t, align_bytes=DMA_ALIGN) for t in range(PACK)]
 
         nc.gpsimd.memset(table_plane[:].bitcast(I32), 0)
         nc.gpsimd.memset(wd_plane_raw[:].bitcast(I32), 0)
@@ -138,7 +140,7 @@ def tile_list_gmlpt_relu_resLP_kernel(
         round_columns(nc.scalar.copy, wg_rounded, wg_raw, 1, 0, M_HALF)
         wg_codes, wg_plane = quantise_weight(wg_rounded, "wg", R // 2)
         early_words = keep.tile(
-            [P, EARLY_WORDS], U32, name="early_words", tag="wg_raw1", align_bytes=64
+            [P, EARLY_WORDS], U32, name="early_words", tag="wg_raw1", align_bytes=DMA_ALIGN
         )
         first = 0
         for width in WORD_GATHERS:
@@ -249,8 +251,8 @@ def tile_list_gmlpt_relu_resLP_kernel(
         hidden_on_vector(6, bank=2)
         quantise_hidden(1)
 
-        y_then_sums = keep.tile([P, Y_PAD + PACK * J], F32, name="y_then_sums")
-        first_sums = keep.tile([P, PACK * OUT_GROUPS[0]], F32, name="first_sums")
+        y_then_sums = keep.tile([P, Y_PAD + PACK * J], F32, name="y_then_sums", align_bytes=DMA_ALIGN)
+        first_sums = keep.tile([P, PACK * OUT_GROUPS[0]], F32, name="first_sums", align_bytes=DMA_ALIGN)
         starts = [sum(OUT_GROUPS[:g]) for g in range(len(OUT_GROUPS))]
 
         def y_slice(group, t):
@@ -288,7 +290,7 @@ def tile_list_gmlpt_relu_resLP_kernel(
 
         out_rows = out_0.rearrange("(p t) j -> p t j", t=PACK)
         out_words = out_1[0].rearrange("p j i -> p (j i)").bitcast(I32)
-        out_plane = keep.tile([P, J], U8, name="out_plane", align_bytes=64)
+        out_plane = keep.tile([P, J], U8, name="out_plane", align_bytes=DMA_ALIGN)
         out_rounded = keep.tile([P, PACK * J], BF16, name="out_rounded", align_bytes=64)
         sums = [first_sums[:].rearrange("p (t j) -> p t j", t=PACK)] + [
             y_then_sums[:, SUMS_AT[g] : SUMS_AT[g] + PACK * OUT_GROUPS[g]].rearrange("p (t j) -> p t j", t=PACK)
@@ -333,7 +335,7 @@ def tile_list_gmlpt_relu_resLP_kernel(
             add_residual(2, t, piece=CHUNK if t == PACK - 1 else None)
         weave(2, CHUNK)
 
-        out_codes = keep.tile([P, J], I32, name="out_codes", align_bytes=64)
+        out_codes = keep.tile([P, J], I32, name="out_codes", align_bytes=DMA_ALIGN)
         first = 0
         stored = 0
         for width in PLANE_GROUPS:

from contextlib import ExitStack

import concourse.mybir as mybir

K, R, N, T, J = 512, 512, 512, 2048, 1024
FLOPS = 2 * J * (2 * K * R + R * N)

F32 = mybir.dt.float32
BF16 = mybir.dt.bfloat16
I32 = mybir.dt.int32
U32 = mybir.dt.uint32
U16 = mybir.dt.uint16
U8 = mybir.dt.uint8
FP8X4 = mybir.dt.float8_e4m3fn_x4
FP4X4 = mybir.dt.float4_e2m1fn_x4
ALU = mybir.AluOpType
ACT = mybir.ActivationFunctionType

P = 128
PACK = 4
LIST_ROWS = 16
BANK = 512
CHUNK = BANK // PACK
HALF = J // 2
M_HALF = P // 2
TABLE_LEAD = 256
WG_SCALAR_COLUMNS = 40
WORD_GATHERS = (128, 128, 256, 128)
EARLY_WORDS = sum(WORD_GATHERS)
WU_SCALAR_COLUMNS = 32
GPSIMD_LAST_TOKENS = 112
OUT_GROUPS = (512, 256, 256)
FIRST_Y_PIECE = 256
PLANE_GROUPS = (512, 256, 128, 128)
WORD_STORE_ENDS = (512, 768, 1024)
DMA_ALIGN = 256
HALF_BYTES = 4 * PACK * R // 2
PLACE_BYTES = 4 * BANK
WU_AT = PLACE_BYTES
LATE_WORDS_AT = 4 * PLACE_BYTES + 64
WD_CODES_AT = LATE_WORDS_AT + 4 * (J - EARLY_WORDS)
AFTER_WU = WD_CODES_AT + 2 * N
PLACES_AT = [32 + u * PLACE_BYTES for u in range(4)] + [AFTER_WU + u * PLACE_BYTES for u in range(4)]
WU_ROUNDED_AT = AFTER_WU + 4 * PLACE_BYTES
WD_PLANE_AT = WU_ROUNDED_AT + 2 * PACK * R - N
OVERLAP = 8
Y_PAD = 2 * OUT_GROUPS[1]
Y_PLACES = ((3, 2, 1, 0), (2, 3, 0, 1), (0, 1, 2, 3))
SUMS_AT = (None, 0, Y_PAD + PACK * OUT_GROUPS[0] - OVERLAP)


def load_scale_rows(queues, plane, rows):
    for r in range(4):
        queues[r % len(queues)].dma_start(
            out=plane[r:P:32, :].bitcast(I32),
            in_=rows[r:16:4, :].bitcast(I32),
        )


def tile_list_gmlpt_relu_resLP_kernel(
    tc, tab_words, tab_scales, wg, wu, wd_words, wd_scales, rT, offs, out_0, out_1, out_2
):
    nc = tc.nc
    with ExitStack() as ctx:
        keep = ctx.enter_context(tc.tile_pool(name="keep", bufs=1))
        after_wu = ctx.enter_context(tc.tile_pool(name="after_wu", bufs=1))
        psum = ctx.enter_context(tc.psum_pool(name="psum", bufs=1))

        offsets = keep.tile([P, J // LIST_ROWS], U16, name="offsets")
        table_words = keep.tile([P, T], I32, name="table_words", align_bytes=DMA_ALIGN)
        table_plane = keep.tile([P, T], U8, name="table_plane", align_bytes=DMA_ALIGN)
        wg_raw = [
            keep.tile([P, PACK, R // 2], F32, name="wg_raw%d" % a, align_bytes=DMA_ALIGN)[:] for a in range(2)
        ]
        first_space = keep.tile([P, BANK + PACK * R // 2], F32, name="first_space", align_bytes=DMA_ALIGN)
        first_place = first_space[:, OVERLAP:]
        wu_raw = [
            first_place[:, BANK - OVERLAP :].rearrange("p (i r) -> p i r", i=PACK),
            after_wu.tile([P, PACK, R // 2], F32, name="wu_raw1", offset=WU_AT + HALF_BYTES, align_bytes=DMA_ALIGN)[:],
        ]
        wd_raw = keep.tile([P, 2 * N], U8, name="wd_raw", align_bytes=DMA_ALIGN)
        wd_plane_raw = keep.tile([P, N], U8, name="wd_plane_raw", align_bytes=DMA_ALIGN)
        residual = [keep.tile([P, T], F32, name="residual%d" % t, align_bytes=DMA_ALIGN) for t in range(PACK)]

        nc.gpsimd.memset(table_plane[:].bitcast(I32), 0)
        nc.gpsimd.memset(wd_plane_raw[:].bitcast(I32), 0)


        def load_half(raw, w, a):
            rows = w.rearrange("(p i) r -> p i r", i=PACK)
            nc.sync.dma_start(out=raw[a], in_=rows[:, :, a * (R // 2) : (a + 1) * (R // 2)])

        load_half(wg_raw, wg, 0)
        nc.sync.dma_start(offsets[:], offs)
        load_scale_rows((nc.sync,), table_plane, tab_scales[0])
        load_half(wg_raw, wg, 1)
        nc.sync.dma_start(
            out=table_words[:], in_=tab_words[0].rearrange("p t i -> p (t i)").bitcast(I32)
        )
        load_scale_rows((nc.sync,), wd_plane_raw, wd_scales[0])
        for a in range(2):
            load_half(wu_raw, wu, a)
        nc.sync.dma_start(out=wd_raw[:].bitcast(I32), in_=wd_words[0].bitcast(I32))
        residual_rows = rT.rearrange("(p t) c -> p t c", t=PACK)
        for t in range(PACK):
            nc.sync.dma_start(out=residual[t][:], in_=residual_rows[:, t, :])

        def list_slice(first, count):
            return offsets[:, first // LIST_ROWS : (first + count) // LIST_ROWS]

        picked_plane = keep.tile([P, J], U8, name="picked_plane", align_bytes=64)
        nc.vector.tensor_copy(picked_plane[:], table_plane[:].indirect(offsets[:]))

        def gather_words(picked, first, count):
            nc.vector.tensor_copy(
                picked, table_words[:].bitcast(U32).indirect(list_slice(first, count))
            )

        def round_columns(copy, rounded, raw, a, first, last, slices=slice(0, PACK)):
            dealt = rounded[:].rearrange("p (t m i) -> p m i t", t=PACK, i=PACK)
            source = raw[a].rearrange("p i (m t) -> p m i t", t=PACK)
            copy(dealt[:, a * M_HALF + first : a * M_HALF + last, :, slices], source[:, first:last, :, slices])

        def quantise_weight(rounded, name, width):
            codes = keep.tile([P, R], U32, name=name + "_codes", align_bytes=64)
            plane = keep.tile([P, R], U8, name=name + "_plane", align_bytes=64)
            for lo in range(0, R, width):
                nc.vector.quantize_mx(
                    out=codes[:, lo : lo + width].bitcast(FP8X4),
                    scales=plane[:, lo : lo + width],
                    in_=rounded[:, PACK * lo : PACK * (lo + width)],
                )
            return codes, plane

        wg_rounded = keep.tile([P, PACK * R], BF16, name="wg_rounded", align_bytes=64)
        wu_rounded = after_wu.tile(
            [P, PACK * R], BF16, name="wu_rounded", offset=WU_ROUNDED_AT, align_bytes=64
        )
        round_columns(nc.scalar.copy, wg_rounded, wg_raw, 0, 0, M_HALF)
        round_columns(nc.scalar.copy, wg_rounded, wg_raw, 1, 0, M_HALF)
        wg_codes, wg_plane = quantise_weight(wg_rounded, "wg", R // 2)
        early_words = keep.tile(
            [P, EARLY_WORDS], U32, name="early_words", tag="wg_raw1", align_bytes=DMA_ALIGN
        )
        first = 0
        for width in WORD_GATHERS:
            gather_words(early_words[:, first : first + width], first, width)
            first = first + width
        wd_plane = keep.tile([P, PACK, P], U8, name="wd_plane", tag="wg_rounded", align_bytes=64)
        nc.gpsimd.tensor_copy(
            wd_plane[:], wd_plane_raw[:].rearrange("p (m t) -> p t m", t=PACK)
        )
        round_columns(nc.scalar.copy, wu_rounded, wu_raw, 0, 0, WU_SCALAR_COLUMNS)
        for t in range(0, PACK, 2):
            round_columns(
                nc.vector.tensor_copy, wu_rounded, wu_raw, 0, WU_SCALAR_COLUMNS, M_HALF, slice(t, t + 2)
            )
        for t in range(0, PACK, 2):
            round_columns(nc.vector.tensor_copy, wu_rounded, wu_raw, 1, 0, M_HALF, slice(t, t + 2))
        wu_codes, wu_plane = quantise_weight(wu_rounded, "wu", R // 2)
        wd_codes = after_wu.tile(
            [P, PACK, 2 * P], U8, name="wd_codes", offset=WU_ROUNDED_AT, align_bytes=64
        )
        nc.gpsimd.tensor_copy(
            wd_codes[:].rearrange("p t (m b) -> p t m b", b=2),
            wd_raw[:].rearrange("p (m t b) -> p t m b", t=PACK, b=2),
        )
        late_words = after_wu.tile(
            [P, J - EARLY_WORDS], U32, name="late_words", offset=LATE_WORDS_AT, align_bytes=64
        )
        gather_words(late_words[:], EARLY_WORDS, J - EARLY_WORDS)


        def first_product(bank, codes, plane, c):
            first = c * CHUNK
            if first < EARLY_WORDS:
                words = early_words[:, first : first + CHUNK]
            else:
                words = late_words[:, first - EARLY_WORDS : first - EARLY_WORDS + CHUNK]
            product = psum.tile([P, PACK, CHUNK], F32, name="product", tag="bank%d" % bank)
            for t in range(PACK):
                nc.tensor.matmul_mx(
                    out=product[:, t, :],
                    lhsT=codes[:, t * P : (t + 1) * P].bitcast(FP8X4),
                    lhsT_scale=plane[:, t * P : (t + 1) * P],
                    rhs=words.bitcast(FP8X4),
                    rhs_scale=picked_plane[:, first : first + CHUNK],
                    start=True,
                    stop=True,
                )
            return product[:].rearrange("p t j -> p j t")

        gates = {}
        h_rounded = keep.tile([P, (J - CHUNK) * PACK], BF16, name="h_rounded", align_bytes=64)
        h_places = h_rounded[:].rearrange("p (j t) -> p j t", t=PACK)
        h_halves = [h_places[:, HALF - CHUNK :, :], h_places[:, :HALF, :]]
        h_codes = keep.tile([P, J], U32, name="h_codes", align_bytes=64)
        h_plane = keep.tile([P, J], U8, name="h_plane", align_bytes=64)

        def h_chunk(c):
            half, inside = divmod(c * CHUNK, HALF)
            return h_halves[half][:, inside : inside + CHUNK, :]

        def woven_tile(name, place):
            if place == 0:
                return first_place[:, :BANK].rearrange("p (j t) -> p j t", t=PACK)
            if place == 1:
                return first_place[:, BANK : 2 * BANK].rearrange("p (j t) -> p j t", t=PACK)
            return after_wu.tile([P, CHUNK, PACK], F32, name=name, offset=PLACES_AT[place])[:]

        def gate(c, bank, place):
            ga = first_product(bank, wg_codes, wg_plane, c)
            gates[c] = woven_tile("gate%d" % c, place)
            nc.scalar.activation(gates[c], ga, ACT.Relu)

        def hidden_on_vector(c, bank):
            ub = first_product(bank, wu_codes, wu_plane, c)
            nc.vector.tensor_tensor(h_chunk(c), gates[c], ub, ALU.mult)

        def hidden_on_gpsimd(c, bank, place, tokens=CHUNK):
            ub = first_product(bank, wu_codes, wu_plane, c)
            ub_woven = woven_tile("up%d" % c, place)
            nc.scalar.copy(ub_woven[:, :tokens], ub[:, :tokens])
            nc.gpsimd.tensor_tensor(h_chunk(c)[:, :tokens], gates[c][:, :tokens], ub_woven[:, :tokens], ALU.mult)
            return ub

        def quantise_hidden(half):
            tokens = slice(half * HALF, (half + 1) * HALF)
            nc.vector.quantize_mx(
                out=h_codes[:, tokens].bitcast(FP8X4),
                scales=h_plane[:, tokens],
                in_=h_halves[half].rearrange("p j t -> p (j t)"),
            )

        gate(0, bank=0, place=0)
        gate(1, bank=1, place=1)
        gate(3, bank=2, place=2)
        hidden_on_gpsimd(3, bank=5, place=4)
        hidden_on_vector(0, bank=4)
        gate(2, bank=3, place=3)
        gate(4, bank=2, place=5)
        hidden_on_vector(1, bank=6)
        hidden_on_vector(2, bank=0)
        gate(7, bank=1, place=6)
        hidden_on_vector(4, bank=3)
        quantise_hidden(0)
        hidden_on_gpsimd(7, bank=7, place=7)
        gate(5, bank=4, place=4)
        gate(6, bank=6, place=2)
        hidden_on_vector(5, bank=5)
        hidden_on_vector(6, bank=2)
        quantise_hidden(1)

        y_then_sums = keep.tile([P, Y_PAD + PACK * J], F32, name="y_then_sums", align_bytes=DMA_ALIGN)
        first_sums = keep.tile([P, PACK * OUT_GROUPS[0]], F32, name="first_sums", align_bytes=DMA_ALIGN)
        starts = [sum(OUT_GROUPS[:g]) for g in range(len(OUT_GROUPS))]

        def y_slice(group, t):
            at = Y_PAD + PACK * starts[group] + Y_PLACES[group][t] * OUT_GROUPS[group]
            return at, y_then_sums[:, at : at + OUT_GROUPS[group]]

        def down(group, t0, bank, piece=BANK):
            width = OUT_GROUPS[group]
            product = psum.tile([P, BANK], F32, name="down", tag="bank%d" % bank)
            pass_width = min(width, piece)
            for lo in range(0, BANK, pass_width):
                u, inside = divmod(lo, width)
                tokens = slice(starts[group] + inside, starts[group] + inside + pass_width)
                nc.tensor.matmul_mx(
                    out=product[:, lo : lo + pass_width],
                    lhsT=wd_codes[:, t0 + u, :].bitcast(FP4X4),
                    lhsT_scale=wd_plane[:, t0 + u, :],
                    rhs=h_codes[:, tokens].bitcast(FP8X4),
                    rhs_scale=h_plane[:, tokens],
                    start=True,
                    stop=True,
                )
            at = y_slice(group, t0)[0]
            for lo in range(0, BANK, piece):
                nc.scalar.copy(y_then_sums[:, at + lo : at + lo + piece], product[:, lo : lo + piece])

        down(0, 0, 0, piece=FIRST_Y_PIECE)
        down(0, 1, 1)
        down(0, 2, 7)
        down(1, 0, 3)
        down(0, 3, 3)
        down(1, 2, 4)
        down(2, 0, 6)
        down(2, 2, 5)

        out_rows = out_0.rearrange("(p t) j -> p t j", t=PACK)
        out_words = out_1[0].rearrange("p j i -> p (j i)").bitcast(I32)
        out_plane = keep.tile([P, J], U8, name="out_plane", align_bytes=DMA_ALIGN)
        out_rounded = keep.tile([P, PACK * J], BF16, name="out_rounded", align_bytes=64)
        sums = [first_sums[:].rearrange("p (t j) -> p t j", t=PACK)] + [
            y_then_sums[:, SUMS_AT[g] : SUMS_AT[g] + PACK * OUT_GROUPS[g]].rearrange("p (t j) -> p t j", t=PACK)
            for g in (1, 2)
        ]

        def add_residual(group, t, piece=None):
            width = OUT_GROUPS[group]
            piece = piece or width
            for lo in range(0, width, piece):
                nc.vector.tensor_tensor(
                    sums[group][:, t, lo : lo + piece],
                    residual[t][:].indirect(list_slice(starts[group] + lo, piece)),
                    y_slice(group, t)[1][:, lo : lo + piece],
                    ALU.add,
                )
            nc.sync.dma_start(
                out=out_rows[:, t, starts[group] : starts[group] + width], in_=sums[group][:, t, :]
            )

        def weave(group, piece):
            for lo in range(0, OUT_GROUPS[group], piece):
                first = starts[group] + lo
                nc.scalar.copy(
                    out_rounded[:, PACK * first : PACK * (first + piece)].rearrange(
                        "p (c i t) -> p c t i", i=4, t=PACK
                    ),
                    sums[group][:, :, lo : lo + piece].rearrange("p t (c i) -> p c t i", i=4),
                )

        add_residual(0, 0, piece=FIRST_Y_PIECE)
        add_residual(0, 1)
        add_residual(0, 2)
        add_residual(1, 0)
        add_residual(1, 1)
        add_residual(0, 3, piece=FIRST_Y_PIECE)
        weave(0, FIRST_Y_PIECE)
        for t in (2, 3):
            add_residual(1, t)
        weave(1, OUT_GROUPS[1])
        for t in range(PACK):
            add_residual(2, t, piece=CHUNK if t == PACK - 1 else None)
        weave(2, CHUNK)

        out_codes = keep.tile([P, J], I32, name="out_codes", align_bytes=DMA_ALIGN)
        first = 0
        stored = 0
        for width in PLANE_GROUPS:
            tokens = slice(first, first + width)
            nc.vector.quantize_mx(
                out=out_codes[:, tokens].bitcast(FP8X4),
                scales=out_plane[:, tokens],
                in_=out_rounded[:, PACK * first : PACK * (first + width)],
            )
            first = first + width
            if first in WORD_STORE_ENDS:
                nc.sync.dma_start(out=out_words[:, stored:first], in_=out_codes[:, stored:first])
                stored = first
        for r in range(4):
            queue = nc.scalar if r % 2 == 0 else nc.sync
            queue.dma_start(
                out=out_2[0][r:16:4, :].bitcast(I32),
                in_=out_plane[r:P:32, :].bitcast(I32),
            )
